import numpy as np, ml_dtypes
CORES = [3,11,19,27,35,43,51,59]
N = 8
BF = ml_dtypes.bfloat16
V, S, P, Q = 1, 2048, 64, 512
def fill(rng, l, cap):
    l = np.minimum(l, cap); e = S - int(np.sum(l)); o = rng.permutation(P); room = (cap - l)[o]; before = np.add.accumulate(room) - room
    l[o] += np.clip(e - before, 0, room); return l
def lens(rng, cap, g):
    c = np.sort(rng.permutation(S - 1)[:P - 1]) + 1
    return fill(rng, np.diff(np.concatenate([[0], c, [S]])), cap)
def put(d, v, g, a, l):
    j = v % V * P; d["frm"][v // V, g, j:j + P] = a; d["ln"][v // V, g, j:j + P] = l
def make(rng, lengths, share):
    d = {"frm": np.zeros((N, 8, V * P), np.int32), "ln": np.zeros((N, 8, V * P), np.int32), "lit": rng.integers(0, 256, (N, 8, Q)).astype(np.int32)}
    for v in range(N * V):
        for g in range(8):
            s = 1.0 if v == 0 else share[v, g]
            l = lengths(rng, Q if s == 1 else S, g); new = (rng.random(P) < s) & (l <= Q)
            put(d, v, g, np.where(new, S + rng.integers(0, np.maximum(Q - l, 0) + 1), rng.integers(0, S - l + 1)), l)
    return d
def setup_inputs(rng):
    return make(rng, lens, np.full((N * V, 8), 0.25))
def setup_inputs_long(rng):
    def lengths(rng, cap, g):
        l = fill(rng, np.ones(P, np.int64), cap)
        return np.sort(l)[::-1].copy() if g == 0 else np.sort(l) if g == 7 else l
    return make(rng, lengths, np.full((N * V, 8), 0.25))
def setup_inputs_ends(rng):
    d = make(rng, lambda rng, cap, g: np.full(P, S // P), np.full((N * V, 8), 0.25))
    k = rng.integers(0, 3, d["frm"].shape); new = d["frm"] >= S
    d["frm"] = np.where(k == 0, np.where(new, S, 0), np.where(k == 1, np.where(new, S + Q, S) - d["ln"], d["frm"])).astype(np.int32)
    return d
def setup_inputs_moves(rng):
    d = setup_inputs(rng)
    for v in range(1, N * V):
        for g in range(8):
            l = lens(rng, S, g); c = np.add.accumulate(l) - l; p = np.arange(P) if g == v % 8 else rng.permutation(P)
            put(d, v, g, c[p], l[p])
    return d
def setup_inputs_spread(rng):
    share = rng.choice(np.array([0, 0.125, 0.5, 1]), (N * V, 8)); share[N * V - 1, 0] = 0; share[N * V - 1, 1] = 1
    d = make(rng, lambda rng, cap, g: fill(rng, 1 + rng.multinomial(S - P, rng.dirichlet(np.full(P, 0.125))), cap), share)
    d["lit"] = np.where(rng.random(d["lit"].shape) < 0.5, 255 * rng.integers(0, 2, d["lit"].shape), d["lit"]).astype(np.int32)
    return d
def check_inputs(d):
    bad = []; a = np.asarray(d["frm"]).astype(np.int64).reshape(N, 8, V, P); l = np.asarray(d["ln"]).astype(np.int64).reshape(N, 8, V, P); t = np.asarray(d["lit"])
    if (l < 1).any() or (np.sum(l, axis=3) != S).any(): bad.append("lengths")
    copied = (a >= 0) & (a + l <= S); new = (a >= S) & (a + l <= S + Q)
    if not (copied | new).all(): bad.append("pieces")
    if not new[0, :, 0].all(): bad.append("version 0")
    if (t < 0).any() or (t > 255).any(): bad.append("literals")
    return bad
def reference(frm, ln, lit):
    y = np.zeros((N, 8, V * S), np.float32); old = np.zeros((8, S), np.int64)
    for v in range(N * V):
        r, k = v // V, v % V; src = np.concatenate([old, lit[r]], axis=1); new = np.zeros((8, S), np.int64)
        for g in range(8):
            a = frm[r, g, k * P:(k + 1) * P]; l = ln[r, g, k * P:(k + 1) * P]; first = np.add.accumulate(l) - l
            new[g] = src[g][np.repeat(a - first, l) + np.arange(S)]
        y[r, :, k * S:(k + 1) * S] = new; old = new
    return {"y": y}

@@ -1,0 +1,394 @@
+from concourse.bass import DstId, RemoteDMATransfer
+from concourse.mybir import dt, AluOpType, AxisListType, ActivationFunctionType
+
+NV = 8
+S = 2048
+Q = 512
+HALF = S // 2
+BW = 136
+IDN = S + Q
+BIG = float(3 * 2 ** 26)
+
+JOIN = {
+    2: (4, 5, 0, 64, "ca", "arrc0", [[7], [6, 5]]),
+    3: (4, 5, 64, 64, "cb", "arrc1", [[7], [6, 5]]),
+    1: (6, 7, 0, 128, "cf", "arrc2", [[7]]),
+}
+
+SCRATCH = {
+    "lni": ("sbuf", [128, 64], "int32"),
+    "fri": ("sbuf", [128, 64], "int32"),
+    "liti": ("sbuf", [128, 32], "int32"),
+    "litb": ("sbuf", [128, 32], "bfloat16"),
+    "lnf": ("sbuf", [128, 64], "float32"),
+    "zf": ("sbuf", [128, 64], "float32"),
+    "stf": ("sbuf", [128, 72], "float32"),
+    "exi": ("sbuf", [128, 72], "int32"),
+    "dlt": ("sbuf", [128, 64], "float32"),
+    "xx": ("sbuf", [128, 576], "bfloat16"),
+    "iom": ("sbuf", [128, 136], "bfloat16"),
+    "qm1": ("sbuf", [128, 32], "bfloat16"),
+    "qm2": ("sbuf", [128, 32], "bfloat16"),
+    "one": ("sbuf", [128, 144], "bfloat16"),
+    "sele": ("sbuf", [128, 8], "bfloat16"),
+    "selo": ("sbuf", [128, 8], "bfloat16"),
+    "cneg": ("sbuf", [128, 128], "bfloat16"),
+    "qrow": ("sbuf", [128, 128], "bfloat16"),
+    "bcp": ("sbuf", [128, 4], "float32"),
+    "bcn": ("sbuf", [128, 4], "float32"),
+    "ap": ("sbuf", [128, 512], "bfloat16"),
+    "am": ("sbuf", [128, 512], "bfloat16"),
+    "bh": ("sbuf", [128, 4 * BW], "bfloat16"),
+    "bl": ("sbuf", [128, 4 * BW], "bfloat16"),
+    "wl": ("sbuf", [128, Q], "bfloat16"),
+    "w0": ("sbuf", [128, S + Q], "bfloat16"),
+    "w1": ("sbuf", [128, S + Q], "bfloat16"),
+    "w2": ("sbuf", [128, S + Q], "bfloat16"),
+    "w3": ("sbuf", [128, S + 2 * Q], "bfloat16"),
+    "w5": ("sbuf", [128, S + 2 * Q], "bfloat16"),
+    "yo": ("sbuf", [128, S], "float32"),
+    "lland": ("dram", [NV, 128, 32], "bfloat16"),
+    "pci": ("sbuf", [128, 8], "int32"),
+    "p15": ("sbuf", [128, 8], "int32"),
+    "h5": ("sbuf", [128, 4], "float32"),
+    "h80": ("sbuf", [128, 4], "float32"),
+    "pm0": ("sbuf", [128, 4], "float32"),
+    "pm1": ("sbuf", [128, 4], "float32"),
+    "lo": ("sbuf", [128, 160], "bfloat16"),
+    "hib": ("sbuf", [128, 160], "bfloat16"),
+    "hi": ("sbuf", [128, 160], "bfloat16"),
+    "hix": ("sbuf", [128, 32], "bfloat16"),
+    "d15": ("sbuf", [128, 144], "bfloat16"),
+    "d14": ("sbuf", [128, 144], "bfloat16"),
+    "e15": ("sbuf", [128, 144], "bfloat16"),
+    "e14": ("sbuf", [128, 144], "bfloat16"),
+    "ee": ("sbuf", [128, 144], "bfloat16"),
+    "idw": ("sbuf", [128, IDN], "bfloat16"),
+    "cw": ("sbuf", [128, S + Q], "bfloat16"),
+    "cr": ("sbuf", [128, S], "bfloat16"),
+    "ca": ("sbuf", [128, 64], "uint16"),
+    "cb": ("sbuf", [128, 64], "uint16"),
+    "cf": ("sbuf", [128, 128], "uint16"),
+    "psm": ("psum", [128, 512], "float32"),
+    "psq": ("psum", [128, 512], "float32"),
+    "pdh": ("psum", [128, 512], "float32"),
+    "pdl": ("psum", [128, 512], "float32"),
+    "pout": ("psum", [128, 512], "float32"),
+    "pjn": ("psum", [128, 512], "float32"),
+}
+for _v in range(NV):
+    SCRATCH["ls%d" % _v] = ("sbuf", [128, 128], "uint16")
+
+NOPS = 112
+SEMAPHORES = (["d_ln", "d_fr", "d_li", "d_y0", "d_y1", "d_id", "d_cw", "loc", "arrc0", "arrc1", "arrc2"]
+              + ["arrk%d" % v for v in range(NV - 1)] + ["arrl%d" % v for v in range(NV)]
+              + ["lit%d" % v for v in range(NV)] + ["op%d" % k for k in range(NOPS)])
+
+
+def rank_program(g, core, T, topo):
+    r = T.rank_of(core)
+    if r is None:
+        return
+    A = AluOpType
+    F = ActivationFunctionType
+    vec, act, pe, syn = g.vector, g.scalar, g.tensor, g.sync
+    queues = {"g": g, "v": vec, "a": act, "p": pe, "s": syn}
+    seen = {}
+    waited = {}
+    marks = []
+    helper = r in JOIN
+
+    def wait(q, *deps):
+        for d in deps:
+            if d is not None and (q, d) not in seen:
+                seen[(q, d)] = True
+                waited[d[0]] = True
+                queues[q].wait_ge(T.sem[d[0]], d[1])
+
+    def mark(ins):
+        name = "op%d" % len(marks)
+        marks.append(name)
+        ins.then_inc(T.sem[name], 1)
+        return (name, 1)
+
+    def arrived(name, src):
+        return (name, len(topo.engines(T.cores[src], core)))
+
+    if r <= 4:
+        stages = [[v] for v in range(r + 1)]
+    else:
+        stages = [[0], [1], [2], [3], [4, 5]] + ([[6]] if r == 6 else [[6, 7]] if r == 7 else [])
+    wins = [T.wl] + [T["w%d" % st[-1]] for st in stages[:-1]]
+    base = [0] + [S] * (len(stages) - 1)
+
+    if r == 0:
+        syn.dma_start(T.liti[:], T.lit[:]).then_inc(T.sem.d_li, 16)
+        act.dma_start(T.lni[0:8, :], T.ln[:]).then_inc(T.sem.d_ln, 16)
+        syn.dma_start(T.fri[0:8, :], T.frm[:]).then_inc(T.sem.d_fr, 16)
+    else:
+        syn.dma_start(T.lni[0:8, :], T.ln[:]).then_inc(T.sem.d_ln, 16)
+        act.dma_start(T.fri[0:8, :], T.frm[:]).then_inc(T.sem.d_fr, 16)
+        syn.dma_start(T.liti[:], T.lit[:]).then_inc(T.sem.d_li, 16)
+
+    m_w = {}
+
+    def zero_window(k):
+        m_w[k] = mark(vec.memset(wins[k][:, base[k]:base[k] + Q * len(stages[k])], 0.0))
+
+    m_one = mark(vec.memset(T.one[:], 1.0))
+    if helper:
+        m_id0 = mark(vec.memset(T.idw[:, 0:IDN // 2], 0.0))
+    else:
+        m_ap = mark(vec.memset(T.ap[:], 0.0))
+    m_q1 = mark(vec.memset(T.qm1[:], -512.0))
+    m_q2 = mark(vec.memset(T.qm2[:], 512.0))
+    m_zf = mark(vec.memset(T.zf[0:8, :], 0.0))
+    m_st = mark(vec.memset(T.stf[0:8, 0:1], -7.5))
+    m_ex = mark(vec.memset(T.exi[0:8, 0:1], 0))
+    m_neg = mark(vec.memset(T.cneg[0:1, :], -2048.0)) if r == 0 else None
+    m_xx = mark(vec.memset(T.xx[0:8, :], 0.0))
+    if helper:
+        m_ap = mark(vec.memset(T.ap[:], 0.0))
+        m_am = mark(vec.memset(T.am[:], 0.0))
+    if r > 0:
+        zero_window(0)
+        zero_window(1)
+    if helper:
+        wait("a", m_id0)
+        m_id1 = mark(act.activation(T.idw[:, IDN // 2:IDN], T.idw[:, 0:IDN // 2], F.Sigmoid, bias=-200.0))
+    else:
+        wait("a", m_ap)
+        m_am = mark(act.activation(T.am[:], T.ap[:], F.Sigmoid, bias=-200.0))
+
+    imp = {"allow_small_or_imprecise_dtypes": True}
+    chain = [None]
+
+    def gp(ins):
+        chain[0] = mark(ins)
+        return chain[0]
+
+    wait("g", m_one)
+    c_sele = gp(g.affine_select(T.sele[0:8, 0:4], T.one[0:8, 0:4], [[-2, 4]], A.is_equal, 0.0, 0, 1))
+    wait("g", chain[0])
+    c_selo = gp(g.affine_select(T.selo[0:8, 0:4], T.one[0:8, 0:4], [[-2, 4]], A.is_equal, 0.0, -1, 1))
+    wait("g", chain[0])
+    c_iom = gp(g.iota(T.iom[:, 0:129], [[16, 129]], -16, 0, **imp))
+    wait("g", chain[0], m_q1)
+    c_q1a = gp(g.iota(T.qm1[0:64, 0:16], [[1, 16]], -7, 0, **imp))
+    wait("g", chain[0])
+    c_q1b = gp(g.iota(T.qm1[64:128, 16:32], [[1, 16]], -7, 0, **imp))
+    wait("g", chain[0], m_q2)
+    c_q2a = gp(g.iota(T.qm2[0:64, 0:16], [[1, 16]], -7, 0, **imp))
+    wait("g", chain[0])
+    c_q2b = gp(g.iota(T.qm2[64:128, 16:32], [[1, 16]], -7, 0, **imp))
+    wait("g", chain[0])
+    c_qrow = gp(g.iota(T.qrow[0:1, :], [[0, 8], [1, 16]], 0, 0, **imp))
+    if helper:
+        wait("g", chain[0])
+        c_pci = gp(g.iota(T.pci[:, 0:1], [[0, 1]], 0, 1))
+        wait("g", chain[0])
+        c_hib = gp(g.iota(T.hib[:], [[1, 5], [0, 32]], 0, 0, **imp))
+        wait("g", chain[0])
+        c_lo = gp(g.iota(T.lo[:], [[0, 5], [1, 32]], 0, 0, **imp))
+
+    def xs(k):
+        return T.xx[0:8, 64 + 128 * k:128 + 128 * k]
+
+    if r == 0:
+        wait("v", ("d_li", 16))
+        o_lb = mark(vec.tensor_copy(T.litb[:], T.liti[:]))
+    wait("v", ("d_ln", 16))
+    o_lnf = mark(vec.tensor_copy(T.lnf[0:8, :], T.lni[0:8, :]))
+    wait("v", ("d_fr", 16), m_ex)
+    o_ex = mark(vec.tensor_tensor(T.exi[0:8, 1:65], T.fri[0:8, :], T.lni[0:8, :], A.add))
+    wait("v", o_lnf, m_st, m_zf)
+    o_st = mark(vec.tensor_tensor_scan(T.stf[0:8, 1:65], T.lnf[0:8, :], T.zf[0:8, :], -7.5, A.add, A.add))
+    wait("v", o_ex, m_xx)
+    o_xh = mark(vec.tensor_tensor(xs(1), T.fri[0:8, :], T.exi[0:8, 0:64], A.subtract))
+    wait("v", o_st)
+    o_xm = mark(vec.tensor_scalar(xs(0), T.stf[0:8, 0:64], BIG, -BIG, A.add, A.add))
+    o_dl = mark(vec.tensor_tensor(T.dlt[0:8, :], T.fri[0:8, :], T.exi[0:8, 0:64], A.subtract))
+    wait("v", o_xm)
+    o_xq = mark(vec.tensor_tensor(xs(2), xs(0), T.stf[0:8, 0:64], A.subtract))
+    wait("v", o_dl, o_xh)
+    o_xl = mark(vec.tensor_tensor(xs(3), T.dlt[0:8, :], xs(1), A.subtract))
+    if r > 0:
+        wait("v", ("d_li", 16))
+        o_lb = mark(vec.tensor_copy(T.litb[:], T.liti[:]))
+
+    wait("p", c_iom, m_one)
+    pe.matmul(T.pout[:, 0:128], T.one[0:1, 0:128], T.iom[0:1, 1:129], True, False)
+    wait("p", c_sele, c_selo, m_xx)
+    p_col = {}
+    for ps, k, dep in (("pdh", 1, o_xh), ("psm", 0, o_xm), ("psq", 2, o_xq), ("pdl", 3, o_xl)):
+        wait("p", dep)
+        pe.matmul(T[ps][:, 0:4], T.xx[0:8, 64 + 128 * k:192 + 128 * k], T.sele[0:8, 0:4], True, False)
+        p_col[ps] = mark(pe.matmul(T[ps][:, 0:4], T.xx[0:8, 128 * k:128 + 128 * k], T.selo[0:8, 0:4], False, True))
+    wait("p", c_qrow, m_neg)
+    pe.matmul(T.pout[:, 0:128], T.qrow[0:1, :], T.one[0:1, 0:128], False, False)
+    if r == 0:
+        pe.matmul(T.pout[:, 0:128], T.cneg[0:1, :], T.one[0:1, 0:128], False, False)
+
+    wait("a", p_col["psq"])
+    a_bp = mark(act.activation(T.bcp[:], T.psq[:, 0:4], F.Identity, scale=256.0))
+    a_bn = mark(act.activation(T.bcn[:], T.psq[:, 0:4], F.Identity, scale=-256.0))
+    wait("a", m_ap, m_am, c_q1a, c_q1b, c_q2a, c_q2b, a_bp, a_bn)
+    a_lf = []
+    for b in range(4):
+        la = mark(act.activation(T.ap[:, 160 * b:160 * b + 32], T.qm1[:], F.Sigmoid, bias=T.bcp[:, b:b + 1], scale=256.0))
+        lb = mark(act.activation(T.am[:, 160 * b:160 * b + 32], T.qm2[:], F.Sigmoid, bias=T.bcn[:, b:b + 1], scale=-256.0))
+        a_lf.append((la, lb))
+    v_b = []
+    wait("v", c_iom, p_col["pdh"], p_col["psm"])
+    for b in range(4):
+        vh = mark(vec.tensor_scalar(T.bh[:, BW * b:BW * b + 129], T.iom[:, 0:129], T.psm[:, b:b + 1], T.pdh[:, b:b + 1],
+                                    A.is_ge, A.mult))
+        wait("v", p_col["pdl"])
+        vl = mark(vec.tensor_scalar(T.bl[:, BW * b:BW * b + 129], T.iom[:, 0:129], T.psm[:, b:b + 1], T.pdl[:, b:b + 1],
+                                    A.is_ge, A.mult))
+        v_b.append((vh, vl))
+    last = None
+    for b in range(4):
+        lp, lm = T.ap[:, 128 * b:128 * b + 128], T.am[:, 128 * b:128 * b + 128]
+        now_h, now_l = T.bh[:, BW * b + 1:BW * b + 129], T.bl[:, BW * b + 1:BW * b + 129]
+        old_h, old_l = T.bh[:, BW * b:BW * b + 128], T.bl[:, BW * b:BW * b + 128]
+        wait("p", v_b[b][0], v_b[b][1], a_lf[b][0])
+        pe.matmul(T.pout[:, 0:128], lp, now_h, False, False)
+        pe.matmul(T.pout[:, 0:128], lp, now_l, False, False)
+        wait("p", a_lf[b][1])
+        pe.matmul(T.pout[:, 0:128], lm, old_h, False, False)
+        last = pe.matmul(T.pout[:, 0:128], lm, old_l, False, b == 3)
+    p_out = mark(last)
+    if helper:
+        wait("v", c_pci)
+        o_p15 = mark(vec.tensor_scalar(T.p15[:, 0:1], T.pci[:, 0:1], 15, None, A.bitwise_and))
+        wait("v", o_p15)
+        o_h5 = mark(vec.tensor_scalar(T.h5[:, 0:1], T.p15[:, 0:1], 5.0, None, A.mult))
+        o_h80 = mark(vec.tensor_scalar(T.h80[:, 0:1], T.p15[:, 0:1], 80.0, None, A.add))
+    own = T["ls%d" % r]
+    wait("v", p_out)
+    o_ls = mark(vec.tensor_copy(own[:], T.pout[:, 0:128]))
+
+    sent = [0]
+
+    def send(src, dst, dests, sem):
+        mask = topo.mask(core, T.cores[dests[0]])
+        ids = []
+        for d in dests:
+            rid, pid, _se = topo.addr(T.cores[d])
+            ids.append(DstId(rid=rid, pnc=pid))
+        g.remote_dma_fused([RemoteDMATransfer(dst_ids=ids, dma_engine_mask=mask, remote_sem=T.sem[sem],
+                                              srcs=[src], dsts=[dst] * len(dests))], local_sem=T.sem.loc)
+        sent[0] += len(topo.engines(core, T.cores[dests[0]]))
+
+    far = [d for d in range(NV - 1, r, -1) if d >= 4]
+    near = [d for d in range(3, r, -1)]
+    if far:
+        wait("g", o_lb)
+        send(T.litb[:], T.lland[r], far, "arrk%d" % r)
+    if helper:
+        wait("g", chain[0])
+        c_d15 = gp(g.affine_select(T.d15[:], T.one[:], [[1, 144]], A.is_equal, 0.0, -15, -1))
+        wait("g", chain[0])
+        c_d14 = gp(g.affine_select(T.d14[:], T.one[:], [[1, 144]], A.is_equal, 0.0, -14, -1))
+    wait("g", o_ls)
+    if r <= 3:
+        for c in ([[7], [6], [5, 4]] if r == 0 else [[7, 6], [5, 4]]):
+            send(own[:], own[:], c, "arrl%d" % r)
+    else:
+        send(own[:], own[:], [h for h in JOIN if r in JOIN[h][0:2]], "arrl%d" % r)
+    if near:
+        send(T.litb[:], T.lland[r], near, "arrk%d" % r)
+        send(own[:], own[:], near, "arrl%d" % r)
+
+    if helper:
+        wait("v", o_p15)
+        o_pm0 = mark(vec.tensor_scalar(T.pm0[:, 0:1], T.p15[:, 0:1], 0.0, None, A.is_equal))
+        o_pm1 = mark(vec.tensor_scalar(T.pm1[:, 0:1], T.p15[:, 0:1], 1.0, 32.0, A.is_equal, A.mult))
+        m_cw = mark(vec.memset(T.cw[:, S:S + Q], 0.0))
+    for k in range(len(stages)):
+        if k not in m_w:
+            zero_window(k)
+    if helper:
+        wait("v", c_d15, c_d14, o_pm0, o_pm1)
+        o_e15 = mark(vec.tensor_scalar(T.e15[:], T.d15[:], T.pm0[:, 0:1], None, A.mult))
+        o_e14 = mark(vec.tensor_scalar(T.e14[:], T.d14[:], T.pm1[:, 0:1], None, A.mult))
+        wait("v", o_e15, o_e14)
+        o_ee = mark(vec.tensor_tensor(T.ee[:], T.e15[:], T.e14[:], A.add))
+        wait("a", c_hib, o_h5)
+        a_hi = mark(act.activation(T.hi[:], T.hib[:], F.Identity, bias=T.h5[:, 0:1]))
+        wait("a", o_h80, m_one)
+        a_hix = mark(act.activation(T.hix[:], T.one[:, 0:32], F.Identity, scale=T.h80[:, 0:1]))
+        wait("s", m_id0, m_id1, c_lo)
+        syn.dma_start(T.idw[0:128:16, :], T.lo[:]).then_inc(T.sem.d_id, 16)
+        wait("s", a_hi)
+        syn.dma_start(T.idw[1:128:16, :], T.hi[:]).then_inc(T.sem.d_id, 16)
+        wait("s", m_cw)
+        syn.dma_start(T.cw[0:128:16, S:S + Q], T.lo[:, 0:32]).then_inc(T.sem.d_cw, 16)
+        wait("s", a_hix)
+        syn.dma_start(T.cw[1:128:16, S:S + Q], T.hix[:]).then_inc(T.sem.d_cw, 16)
+
+    for k in range(len(stages)):
+        for n, v in enumerate(stages[k]):
+            at = base[k] + Q * n
+            dst = wins[k][0:128:16, at:at + Q]
+            wait("s", m_w[k])
+            if v == r:
+                wait("s", o_lb)
+                syn.dma_start(dst, T.litb[:]).then_inc(T.sem["lit%d" % v], 16)
+            else:
+                wait("s", arrived("arrk%d" % v, v))
+                syn.dma_start(dst, T.lland[v]).then_inc(T.sem["lit%d" % v], 16)
+
+    if helper:
+        v0, v1, c0, nc, buf, sem, calls = JOIN[r]
+        l0, l1 = T["ls%d" % v0], T["ls%d" % v1]
+        half = nc // 2
+        for q in ("v", "a"):
+            wait(q, ("d_id", 32), arrived("arrl%d" % v0, v0))
+        i_v = mark(vec.tensor_copy(T.cw[:, 0:HALF], T.idw[:].indirect(l0[:, 0:64])))
+        i_a = mark(act.activation(T.cw[:, HALF:S], T.idw[:].indirect(l0[:, 64:128]), F.Copy))
+        for q in ("v", "a"):
+            wait(q, i_v, i_a, ("d_cw", 32), arrived("arrl%d" % v1, v1))
+        j_v = mark(vec.tensor_copy(T.cr[:, 0:16 * half], T.cw[:].indirect(l1[:, c0:c0 + half])))
+        j_a = mark(act.activation(T.cr[:, 16 * half:16 * nc], T.cw[:].indirect(l1[:, c0 + half:c0 + nc]), F.Copy))
+        wait("p", o_ee, j_v, j_a)
+        for q in range(16):
+            last = pe.matmul(T.pjn[:, 0:nc], T.ee[:, 15 - q:143 - q], T.cr[:, q:16 * nc:16], q == 0, q == 15)
+        p_jn = mark(last)
+        wait("v", p_jn)
+        o_jn = mark(vec.tensor_copy(T[buf][:], T.pjn[:, 0:nc]))
+        wait("g", o_jn)
+        for c in calls:
+            send(T[buf][:], T[buf][:], c, sem)
+
+    prev = []
+    for k, st in enumerate(stages):
+        v = st[-1]
+        win = wins[k][:, 0:base[k] + Q * len(st)]
+        out = T.yo if k == len(stages) - 1 else wins[k + 1]
+        if len(st) == 1:
+            lst = T["ls%d" % v]
+            lists = (lst[:, 0:64], lst[:, 64:128])
+            got = [o_ls if v == r else arrived("arrl%d" % v, v)] * 2
+        elif v == 5:
+            lists = (T.ca[:], T.cb[:])
+            got = [arrived("arrc0", 2), arrived("arrc1", 3)]
+        else:
+            lists = (T.cf[:, 0:64], T.cf[:, 64:128])
+            got = [arrived("arrc2", 1)] * 2
+        lits = [("lit%d" % x, 16) for x in st]
+        wait("v", *lits, got[0], *prev)
+        wait("a", *lits, got[1], *prev)
+        prev = [mark(vec.tensor_copy(out[:, 0:HALF], win.indirect(lists[0]))),
+                mark(act.activation(out[:, HALF:S], win.indirect(lists[1]), F.Copy))]
+    wait("s", prev[0])
+    syn.dma_start(T.y[:, 0:HALF], T.yo[0:128:16, 0:HALF]).then_inc(T.sem.d_y0, 16)
+    wait("a", prev[1])
+    act.dma_start(T.y[:, HALF:S], T.yo[0:128:16, HALF:S]).then_inc(T.sem.d_y1, 16)
+    wait("g", ("loc", sent[0]))
+    wait("s", ("d_y0", 16))
+    wait("a", ("d_y1", 16))
+    for name in marks:
+        if name not in waited:
+            wait("s", (name, 1))

@@ -4,85 +4,79 @@ from concourse.mybir import dt, AluOpType, AxisListType, ActivationFunctionType
 NV = 8
 S = 2048
 Q = 512
-HALF = S // 2
-BW = 136
-IDN = S + Q
-BIG = float(3 * 2 ** 26)
-
-JOIN = {
-    2: (4, 5, 0, 64, "ca", "arrc0", [[7], [6, 5]]),
-    3: (4, 5, 64, 64, "cb", "arrc1", [[7], [6, 5]]),
-    1: (6, 7, 0, 128, "cf", "arrc2", [[7]]),
-}
+BW = 36
+UW = 384
+MW = S + 2 * Q
+J = 3
+BIG128 = float(3 * 2 ** 29)
+BIG32 = float(3 * 2 ** 27)
+WIN = {1: (0, 160), 2: (160, 160), 3: (320, 192), 5: (512, 192), 7: (704, 160)}
+CHAIN = [(0, 0, 0, 1), (1, 1, 1, 2), (2, 2, 2, 3), (4, 8, 3, 5), (6, 9, 5, 7), (7, 7, 7, None)]
+HALVES = (8, 9)
+CALLS = [[v] for v in range(NV)]
+VFIRST, AFIRST = ["lf", "low1", "lows", "lit0"], ["m4", "jw0", "jw1", "m1"]
+VSLOT = [["j0", "|", "lit1"], ["j1", "|", "c0"], ["y0", "y1", "c1", "|", "y2"], ["v3", "|"], ["v5", "|"]]
+ASLOT = [["m6", "m2"], ["m3", "m8"], ["m9"], ["m5", "m7", "Y4", "Y3"], ["Y6", "Y5"]]
 
 SCRATCH = {
     "lni": ("sbuf", [128, 64], "int32"),
     "fri": ("sbuf", [128, 64], "int32"),
-    "liti": ("sbuf", [128, 32], "int32"),
-    "litb": ("sbuf", [128, 32], "bfloat16"),
-    "lnf": ("sbuf", [128, 64], "float32"),
     "zf": ("sbuf", [128, 64], "float32"),
-    "stf": ("sbuf", [128, 72], "float32"),
-    "exi": ("sbuf", [128, 72], "int32"),
-    "dlt": ("sbuf", [128, 64], "float32"),
-    "xx": ("sbuf", [128, 576], "bfloat16"),
-    "iom": ("sbuf", [128, 136], "bfloat16"),
-    "qm1": ("sbuf", [128, 32], "bfloat16"),
-    "qm2": ("sbuf", [128, 32], "bfloat16"),
-    "one": ("sbuf", [128, 144], "bfloat16"),
-    "sele": ("sbuf", [128, 8], "bfloat16"),
-    "selo": ("sbuf", [128, 8], "bfloat16"),
-    "cneg": ("sbuf", [128, 128], "bfloat16"),
-    "qrow": ("sbuf", [128, 128], "bfloat16"),
-    "bcp": ("sbuf", [128, 4], "float32"),
-    "bcn": ("sbuf", [128, 4], "float32"),
-    "ap": ("sbuf", [128, 512], "bfloat16"),
-    "am": ("sbuf", [128, 512], "bfloat16"),
-    "bh": ("sbuf", [128, 4 * BW], "bfloat16"),
-    "bl": ("sbuf", [128, 4 * BW], "bfloat16"),
-    "wl": ("sbuf", [128, Q], "bfloat16"),
-    "w0": ("sbuf", [128, S + Q], "bfloat16"),
-    "w1": ("sbuf", [128, S + Q], "bfloat16"),
-    "w2": ("sbuf", [128, S + Q], "bfloat16"),
-    "w3": ("sbuf", [128, S + 2 * Q], "bfloat16"),
-    "w5": ("sbuf", [128, S + 2 * Q], "bfloat16"),
-    "yo": ("sbuf", [128, S], "float32"),
-    "lland": ("dram", [NV, 128, 32], "bfloat16"),
-    "pci": ("sbuf", [128, 8], "int32"),
-    "p15": ("sbuf", [128, 8], "int32"),
-    "h5": ("sbuf", [128, 4], "float32"),
-    "h80": ("sbuf", [128, 4], "float32"),
-    "pm0": ("sbuf", [128, 4], "float32"),
-    "pm1": ("sbuf", [128, 4], "float32"),
-    "lo": ("sbuf", [128, 160], "bfloat16"),
-    "hib": ("sbuf", [128, 160], "bfloat16"),
-    "hi": ("sbuf", [128, 160], "bfloat16"),
-    "hix": ("sbuf", [128, 32], "bfloat16"),
-    "d15": ("sbuf", [128, 144], "bfloat16"),
-    "d14": ("sbuf", [128, 144], "bfloat16"),
-    "e15": ("sbuf", [128, 144], "bfloat16"),
-    "e14": ("sbuf", [128, 144], "bfloat16"),
+    "xx": ("sbuf", [128, 576], "float16"),
+    "one": ("sbuf", [128, 128], "bfloat16"),
+    "sel": ("sbuf", [128, 8], "bfloat16"),
+    "seln": ("sbuf", [128, 8], "bfloat16"),
+    "fine": ("sbuf", [128, 128], "bfloat16"),
+    "rr": ("sbuf", [128, 48], "bfloat16"),
+    "thr": ("sbuf", [128, 48], "bfloat16"),
+    "krow": ("sbuf", [128, 48], "bfloat16"),
+    "chalf": ("sbuf", [128, 128], "bfloat16"),
+    "seed": ("sbuf", [128, 16], "bfloat16"),
+    "cc": ("sbuf", [128, UW // 16], "bfloat16"),
+    "cols": ("sbuf", [128, 8], "float32"),
+    "lp": ("sbuf", [128, 512], "bfloat16"),
+    "lm": ("sbuf", [128, 512], "bfloat16"),
+    "bf": ("sbuf", [128, 4 * BW], "float16"),
+    "be": ("sbuf", [128, 4 * BW], "float16"),
+    "snd": ("sbuf", [128, 4 * 40], "uint16"),
+    "lst": ("sbuf", [128, 160], "uint16"),
+    "low": ("sbuf", [128, 160], "uint16"),
+    "rep": ("sbuf", [128, UW // 16], "uint16"),
+    "mw": ("sbuf", [128, MW], "bfloat16"),
+    "ident": ("sbuf", [128, 128], "bfloat16"),
+    "rlh": ("sbuf", [128, 16], "bfloat16"),
+    "rl": ("sbuf", [128, 160], "bfloat16"),
+    "w0": ("sbuf", [128, Q], "int32"),
+    "lt0": ("sbuf", [128, 16], "int32"),
+    "lt1": ("sbuf", [128, 16], "int32"),
+    "lrep": ("sbuf", [128, 64], "bfloat16"),
+    "win": ("sbuf", [128, 864], "bfloat16"),
+    "msk": ("sbuf", [128, 10 * 256], "bfloat16"),
+    "res": ("sbuf", [128, NV * 256], "bfloat16"),
+    "yo": ("sbuf", [128, NV * 16], "float32"),
+    "frow": ("sbuf", [128, 128], "bfloat16"),
+    "pick": ("sbuf", [128, 1024], "bfloat16"),
     "ee": ("sbuf", [128, 144], "bfloat16"),
-    "idw": ("sbuf", [128, IDN], "bfloat16"),
-    "cw": ("sbuf", [128, S + Q], "bfloat16"),
-    "cr": ("sbuf", [128, S], "bfloat16"),
-    "ca": ("sbuf", [128, 64], "uint16"),
-    "cb": ("sbuf", [128, 64], "uint16"),
-    "cf": ("sbuf", [128, 128], "uint16"),
-    "psm": ("psum", [128, 512], "float32"),
-    "psq": ("psum", [128, 512], "float32"),
-    "pdh": ("psum", [128, 512], "float32"),
-    "pdl": ("psum", [128, 512], "float32"),
-    "pout": ("psum", [128, 512], "float32"),
-    "pjn": ("psum", [128, 512], "float32"),
+    "lf": ("sbuf", [128, 48], "float16"),
+    "jw": ("sbuf", [128, 320], "float32"),
+    "rj": ("sbuf", [128, 512], "float16"),
+    "stg": ("dram", [NV, 128, 4], "int32"),
+    "land": ("dram", [NV, 128, 4], "int32"),
+    "yl": ("dram", [NV, 128, 16], "float32"),
+    "pq": ("psum", [128, 512], "float32"),
+    "po0": ("psum", [128, 512], "float32"),
+    "po1": ("psum", [128, 512], "float32"),
+    "po2": ("psum", [128, 512], "float32"),
+    "po3": ("psum", [128, 512], "float32"),
+    "pj": ("psum", [128, 512], "float32"),
+    "pwa": ("psum", [128, 512], "float32"),
+    "pwb": ("psum", [128, 512], "float32"),
 }
-for _v in range(NV):
-    SCRATCH["ls%d" % _v] = ("sbuf", [128, 128], "uint16")
 
-NOPS = 112
-SEMAPHORES = (["d_ln", "d_fr", "d_li", "d_y0", "d_y1", "d_id", "d_cw", "loc", "arrc0", "arrc1", "arrc2"]
-              + ["arrk%d" % v for v in range(NV - 1)] + ["arrl%d" % v for v in range(NV)]
-              + ["lit%d" % v for v in range(NV)] + ["op%d" % k for k in range(NOPS)])
+NOPS = 110
+SEMAPHORES = (["d_ln", "d_fr", "d_stg", "d_own", "d_w0", "d_lt0", "d_lt1", "d_y", "loc", "arrk0", "arrka", "arrkb",
+               "arrl0", "arrl1", "arrl", "arry", "g1", "g2", "pa", "pb", "ca", "cb", "mw", "lr0", "lr1", "sel", "thr",
+               "pick", "js", "f0", "f1", "f2", "f3"] + ["op%d" % k for k in range(NOPS)])
 
 
 def rank_program(g, core, T, topo):
@@ -95,300 +89,426 @@ def rank_program(g, core, T, topo):
     queues = {"g": g, "v": vec, "a": act, "p": pe, "s": syn}
     seen = {}
     waited = {}
+    total = {}
     marks = []
-    helper = r in JOIN
 
     def wait(q, *deps):
         for d in deps:
-            if d is not None and (q, d) not in seen:
-                seen[(q, d)] = True
-                waited[d[0]] = True
+            if d is not None and d[1] > 0 and seen.get((q, d[0]), 0) < d[1]:
+                seen[(q, d[0])] = d[1]
+                waited[d[0]] = max(waited.get(d[0], 0), d[1])
                 queues[q].wait_ge(T.sem[d[0]], d[1])
+
+    def count(ins, name, n=1):
+        total[name] = total.get(name, 0) + n
+        ins.then_inc(T.sem[name], n)
+        return (name, total[name])
 
     def mark(ins):
         name = "op%d" % len(marks)
         marks.append(name)
-        ins.then_inc(T.sem[name], 1)
-        return (name, 1)
+        return count(ins, name)
 
-    def arrived(name, src):
-        return (name, len(topo.engines(T.cores[src], core)))
+    def shares(src, dests):
+        eng = topo.engines(T.cores[src], T.cores[dests[0]])
+        n = [1] * len(dests)
+        k = len(dests) - 1
+        while sum(n) + n[k] <= len(eng):
+            n[k] *= 2
+            k = (k - 1) % len(dests)
+        out, at = {}, 0
+        for d, m in zip(dests, n):
+            out[d] = eng[at:at + m]
+            at += m
+        return out
 
-    if r <= 4:
-        stages = [[v] for v in range(r + 1)]
-    else:
-        stages = [[0], [1], [2], [3], [4, 5]] + ([[6]] if r == 6 else [[6, 7]] if r == 7 else [])
-    wins = [T.wl] + [T["w%d" % st[-1]] for st in stages[:-1]]
-    base = [0] + [S] * (len(stages) - 1)
+    def others(src):
+        return [d for d in range(NV) if d != src]
 
-    if r == 0:
-        syn.dma_start(T.liti[:], T.lit[:]).then_inc(T.sem.d_li, 16)
-        act.dma_start(T.lni[0:8, :], T.ln[:]).then_inc(T.sem.d_ln, 16)
-        syn.dma_start(T.fri[0:8, :], T.frm[:]).then_inc(T.sem.d_fr, 16)
-    else:
-        syn.dma_start(T.lni[0:8, :], T.ln[:]).then_inc(T.sem.d_ln, 16)
-        act.dma_start(T.fri[0:8, :], T.frm[:]).then_inc(T.sem.d_fr, 16)
-        syn.dma_start(T.liti[:], T.lit[:]).then_inc(T.sem.d_li, 16)
+    def docs(src):
+        return list(range(NV)) if src >= 2 else others(src) + [src]
 
-    m_w = {}
+    def pairs(src):
+        out = []
+        for b in range(4):
+            two = docs(src)[2 * b:2 * b + 2]
+            calls = [two[0:1], two[1:2]] if b == 3 else [two]
+            calls = [[d for d in c if d != src] for c in calls]
+            out.append((b, [c for c in calls if c]))
+        return out
 
-    def zero_window(k):
-        m_w[k] = mark(vec.memset(wins[k][:, base[k]:base[k] + Q * len(stages[k])], 0.0))
-
-    m_one = mark(vec.memset(T.one[:], 1.0))
-    if helper:
-        m_id0 = mark(vec.memset(T.idw[:, 0:IDN // 2], 0.0))
-    else:
-        m_ap = mark(vec.memset(T.ap[:], 0.0))
-    m_q1 = mark(vec.memset(T.qm1[:], -512.0))
-    m_q2 = mark(vec.memset(T.qm2[:], 512.0))
-    m_zf = mark(vec.memset(T.zf[0:8, :], 0.0))
-    m_st = mark(vec.memset(T.stf[0:8, 0:1], -7.5))
-    m_ex = mark(vec.memset(T.exi[0:8, 0:1], 0))
-    m_neg = mark(vec.memset(T.cneg[0:1, :], -2048.0)) if r == 0 else None
-    m_xx = mark(vec.memset(T.xx[0:8, :], 0.0))
-    if helper:
-        m_ap = mark(vec.memset(T.ap[:], 0.0))
-        m_am = mark(vec.memset(T.am[:], 0.0))
-    if r > 0:
-        zero_window(0)
-        zero_window(1)
-    if helper:
-        wait("a", m_id0)
-        m_id1 = mark(act.activation(T.idw[:, IDN // 2:IDN], T.idw[:, 0:IDN // 2], F.Sigmoid, bias=-200.0))
-    else:
-        wait("a", m_ap)
-        m_am = mark(act.activation(T.am[:], T.ap[:], F.Sigmoid, bias=-200.0))
-
-    imp = {"allow_small_or_imprecise_dtypes": True}
-    chain = [None]
-
-    def gp(ins):
-        chain[0] = mark(ins)
-        return chain[0]
-
-    wait("g", m_one)
-    c_sele = gp(g.affine_select(T.sele[0:8, 0:4], T.one[0:8, 0:4], [[-2, 4]], A.is_equal, 0.0, 0, 1))
-    wait("g", chain[0])
-    c_selo = gp(g.affine_select(T.selo[0:8, 0:4], T.one[0:8, 0:4], [[-2, 4]], A.is_equal, 0.0, -1, 1))
-    wait("g", chain[0])
-    c_iom = gp(g.iota(T.iom[:, 0:129], [[16, 129]], -16, 0, **imp))
-    wait("g", chain[0], m_q1)
-    c_q1a = gp(g.iota(T.qm1[0:64, 0:16], [[1, 16]], -7, 0, **imp))
-    wait("g", chain[0])
-    c_q1b = gp(g.iota(T.qm1[64:128, 16:32], [[1, 16]], -7, 0, **imp))
-    wait("g", chain[0], m_q2)
-    c_q2a = gp(g.iota(T.qm2[0:64, 0:16], [[1, 16]], -7, 0, **imp))
-    wait("g", chain[0])
-    c_q2b = gp(g.iota(T.qm2[64:128, 16:32], [[1, 16]], -7, 0, **imp))
-    wait("g", chain[0])
-    c_qrow = gp(g.iota(T.qrow[0:1, :], [[0, 8], [1, 16]], 0, 0, **imp))
-    if helper:
-        wait("g", chain[0])
-        c_pci = gp(g.iota(T.pci[:, 0:1], [[0, 1]], 0, 1))
-        wait("g", chain[0])
-        c_hib = gp(g.iota(T.hib[:], [[1, 5], [0, 32]], 0, 0, **imp))
-        wait("g", chain[0])
-        c_lo = gp(g.iota(T.lo[:], [[0, 5], [1, 32]], 0, 0, **imp))
-
-    def xs(k):
-        return T.xx[0:8, 64 + 128 * k:128 + 128 * k]
-
-    if r == 0:
-        wait("v", ("d_li", 16))
-        o_lb = mark(vec.tensor_copy(T.litb[:], T.liti[:]))
-    wait("v", ("d_ln", 16))
-    o_lnf = mark(vec.tensor_copy(T.lnf[0:8, :], T.lni[0:8, :]))
-    wait("v", ("d_fr", 16), m_ex)
-    o_ex = mark(vec.tensor_tensor(T.exi[0:8, 1:65], T.fri[0:8, :], T.lni[0:8, :], A.add))
-    wait("v", o_lnf, m_st, m_zf)
-    o_st = mark(vec.tensor_tensor_scan(T.stf[0:8, 1:65], T.lnf[0:8, :], T.zf[0:8, :], -7.5, A.add, A.add))
-    wait("v", o_ex, m_xx)
-    o_xh = mark(vec.tensor_tensor(xs(1), T.fri[0:8, :], T.exi[0:8, 0:64], A.subtract))
-    wait("v", o_st)
-    o_xm = mark(vec.tensor_scalar(xs(0), T.stf[0:8, 0:64], BIG, -BIG, A.add, A.add))
-    o_dl = mark(vec.tensor_tensor(T.dlt[0:8, :], T.fri[0:8, :], T.exi[0:8, 0:64], A.subtract))
-    wait("v", o_xm)
-    o_xq = mark(vec.tensor_tensor(xs(2), xs(0), T.stf[0:8, 0:64], A.subtract))
-    wait("v", o_dl, o_xh)
-    o_xl = mark(vec.tensor_tensor(xs(3), T.dlt[0:8, :], xs(1), A.subtract))
-    if r > 0:
-        wait("v", ("d_li", 16))
-        o_lb = mark(vec.tensor_copy(T.litb[:], T.liti[:]))
-
-    wait("p", c_iom, m_one)
-    pe.matmul(T.pout[:, 0:128], T.one[0:1, 0:128], T.iom[0:1, 1:129], True, False)
-    wait("p", c_sele, c_selo, m_xx)
-    p_col = {}
-    for ps, k, dep in (("pdh", 1, o_xh), ("psm", 0, o_xm), ("psq", 2, o_xq), ("pdl", 3, o_xl)):
-        wait("p", dep)
-        pe.matmul(T[ps][:, 0:4], T.xx[0:8, 64 + 128 * k:192 + 128 * k], T.sele[0:8, 0:4], True, False)
-        p_col[ps] = mark(pe.matmul(T[ps][:, 0:4], T.xx[0:8, 128 * k:128 + 128 * k], T.selo[0:8, 0:4], False, True))
-    wait("p", c_qrow, m_neg)
-    pe.matmul(T.pout[:, 0:128], T.qrow[0:1, :], T.one[0:1, 0:128], False, False)
-    if r == 0:
-        pe.matmul(T.pout[:, 0:128], T.cneg[0:1, :], T.one[0:1, 0:128], False, False)
-
-    wait("a", p_col["psq"])
-    a_bp = mark(act.activation(T.bcp[:], T.psq[:, 0:4], F.Identity, scale=256.0))
-    a_bn = mark(act.activation(T.bcn[:], T.psq[:, 0:4], F.Identity, scale=-256.0))
-    wait("a", m_ap, m_am, c_q1a, c_q1b, c_q2a, c_q2b, a_bp, a_bn)
-    a_lf = []
-    for b in range(4):
-        la = mark(act.activation(T.ap[:, 160 * b:160 * b + 32], T.qm1[:], F.Sigmoid, bias=T.bcp[:, b:b + 1], scale=256.0))
-        lb = mark(act.activation(T.am[:, 160 * b:160 * b + 32], T.qm2[:], F.Sigmoid, bias=T.bcn[:, b:b + 1], scale=-256.0))
-        a_lf.append((la, lb))
-    v_b = []
-    wait("v", c_iom, p_col["pdh"], p_col["psm"])
-    for b in range(4):
-        vh = mark(vec.tensor_scalar(T.bh[:, BW * b:BW * b + 129], T.iom[:, 0:129], T.psm[:, b:b + 1], T.pdh[:, b:b + 1],
-                                    A.is_ge, A.mult))
-        wait("v", p_col["pdl"])
-        vl = mark(vec.tensor_scalar(T.bl[:, BW * b:BW * b + 129], T.iom[:, 0:129], T.psm[:, b:b + 1], T.pdl[:, b:b + 1],
-                                    A.is_ge, A.mult))
-        v_b.append((vh, vl))
-    last = None
-    for b in range(4):
-        lp, lm = T.ap[:, 128 * b:128 * b + 128], T.am[:, 128 * b:128 * b + 128]
-        now_h, now_l = T.bh[:, BW * b + 1:BW * b + 129], T.bl[:, BW * b + 1:BW * b + 129]
-        old_h, old_l = T.bh[:, BW * b:BW * b + 128], T.bl[:, BW * b:BW * b + 128]
-        wait("p", v_b[b][0], v_b[b][1], a_lf[b][0])
-        pe.matmul(T.pout[:, 0:128], lp, now_h, False, False)
-        pe.matmul(T.pout[:, 0:128], lp, now_l, False, False)
-        wait("p", a_lf[b][1])
-        pe.matmul(T.pout[:, 0:128], lm, old_h, False, False)
-        last = pe.matmul(T.pout[:, 0:128], lm, old_l, False, b == 3)
-    p_out = mark(last)
-    if helper:
-        wait("v", c_pci)
-        o_p15 = mark(vec.tensor_scalar(T.p15[:, 0:1], T.pci[:, 0:1], 15, None, A.bitwise_and))
-        wait("v", o_p15)
-        o_h5 = mark(vec.tensor_scalar(T.h5[:, 0:1], T.p15[:, 0:1], 5.0, None, A.mult))
-        o_h80 = mark(vec.tensor_scalar(T.h80[:, 0:1], T.p15[:, 0:1], 80.0, None, A.add))
-    own = T["ls%d" % r]
-    wait("v", p_out)
-    o_ls = mark(vec.tensor_copy(own[:], T.pout[:, 0:128]))
-
-    sent = [0]
-
-    def send(src, dst, dests, sem):
-        mask = topo.mask(core, T.cores[dests[0]])
-        ids = []
-        for d in dests:
+    def send(pieces, engines, sem):
+        tr = []
+        for d, src, dst in pieces:
             rid, pid, _se = topo.addr(T.cores[d])
-            ids.append(DstId(rid=rid, pnc=pid))
-        g.remote_dma_fused([RemoteDMATransfer(dst_ids=ids, dma_engine_mask=mask, remote_sem=T.sem[sem],
-                                              srcs=[src], dsts=[dst] * len(dests))], local_sem=T.sem.loc)
-        sent[0] += len(topo.engines(core, T.cores[dests[0]]))
+            tr.append(RemoteDMATransfer(dst_ids=[DstId(rid=rid, pnc=pid)], dma_engine_mask=sum(1 << e for e in engines[d]),
+                                        remote_sem=T.sem[sem], srcs=[src], dsts=[dst]))
+            total["loc"] = total.get("loc", 0) + len(engines[d])
+        g.remote_dma_fused(tr, local_sem=T.sem.loc)
 
-    far = [d for d in range(NV - 1, r, -1) if d >= 4]
-    near = [d for d in range(3, r, -1)]
-    if far:
-        wait("g", o_lb)
-        send(T.litb[:], T.lland[r], far, "arrk%d" % r)
-    if helper:
-        wait("g", chain[0])
-        c_d15 = gp(g.affine_select(T.d15[:], T.one[:], [[1, 144]], A.is_equal, 0.0, -15, -1))
-        wait("g", chain[0])
-        c_d14 = gp(g.affine_select(T.d14[:], T.one[:], [[1, 144]], A.is_equal, 0.0, -14, -1))
-    wait("g", o_ls)
-    if r <= 3:
-        for c in ([[7], [6], [5, 4]] if r == 0 else [[7, 6], [5, 4]]):
-            send(own[:], own[:], c, "arrl%d" % r)
+    def lit_in(vs):
+        return sum(len(shares(v, others(v))[r]) for v in vs if v != r)
+
+    def list_in(vs):
+        return sum(len(shares(v, c)[r]) for v in vs if v != r for _b, calls in pairs(v) for c in calls if r in c)
+
+    def lit_sem(v):
+        return "arrk0" if v == 0 else "arrka" if v < 4 else "arrkb"
+
+    def list_sem(v):
+        return "arrl0" if v == 0 else "arrl1" if v == 1 else "arrl"
+
+    d_stg = count(syn.dma_start(T.stg[:], T.lit[:]), "d_stg", 16)
+    d_ln = count(act.dma_start(T.lni[0:8, :], T.ln[:]), "d_ln", 16)
+    d_fr = count(syn.dma_start(T.fri[0:8, :], T.frm[:]), "d_fr", 16)
+    d_own = count(syn.dma_start(T.land[r], T.lit[r]), "d_own", 16)
+
+    def xs(k, a=0, b=64):
+        return T.xx[0:8, 64 + 128 * k + a:64 + 128 * k + b]
+
+    XF, XE, XT, XM = 0, 1, 2, 3
+    imp = {"allow_small_or_imprecise_dtypes": True}
+    m_one = mark(vec.memset(T.one[:], 1.0))
+    zc, hc, uc, pc, ja, jb = [T.cols[:, k:k + 1] for k in range(6)]
+    c_z = mark(g.iota(zc, [[0, 1]], -15 - 256, 2, **imp))
+    c_fine = mark(g.iota(T.fine[:], [[1, 8], [8, 16]], -64, 0, **imp))
+    c_rr = mark(g.iota(T.rr[:, 0:BW], [[0, 2], [128, 18]], -128, 0, **imp))
+    wait("g", m_one)
+    mine = docs(r)
+    cuts = [i for i in range(NV) if i == 0 or mine[i] != mine[i - 1] + 1] + [NV]
+    for a, b in zip(cuts, cuts[1:]):
+        c_sel = count(g.affine_select(T.sel[0:8, a:b], T.one[0:8, a:b], [[-1, b - a]], A.is_equal, 0.0, -mine[a], 1), "sel")
+
+    def first_row():
+        return mark(g.iota(T.frow[:], [[0, 8], [1, 2], [16, 8]], 0, 0, **imp))
+
+    if r >= 2:
+        c_fr = first_row()
+    m_c0 = mark(vec.memset(T.cc[:], 16.0))
+    m_xx = mark(vec.memset(T.xx[0:8, :], 0.0))
+    wait("v", c_z)
+    o_h = mark(vec.tensor_scalar(hc, zc, BIG32, -BIG32, A.add, A.add))
+    wait("v", m_xx)
+    m_t0 = mark(vec.memset(xs(XT, 0, 1), -64.0))
+    m_e0 = mark(vec.memset(xs(XE, 0, 1), (S if r == 0 else 0) - 1280.0))
+    wait("v", o_h)
+    o_u = mark(vec.tensor_scalar(uc, zc, hc, -1.0, A.subtract, A.add))
+    wait("v", c_fine, m_c0)
+    o_rs = mark(vec.tensor_scalar(T.rlh[:], T.fine[:, 0:16], 4.0, hc, A.mult, A.is_equal))
+    wait("v", o_u)
+    o_seed = mark(vec.tensor_scalar(T.seed[:], T.fine[:, 0:16], 0.25, uc, A.mult, A.is_equal))
+    o_rep = mark(vec.tensor_scalar(T.rep[:], T.cc[:], uc, 0.5, A.add, A.mult))
+    o_col = []
+
+    def join_columns():
+        o_col.append(mark(vec.tensor_scalar(pc, zc, 271.0, 0.5, A.add, A.mult)))
+        o_col.append(mark(vec.tensor_scalar(ja, uc, 0.5, 1672.0, A.mult, A.add)))
+        o_col.append(mark(vec.tensor_scalar(jb, uc, 0.5, 1672.0 + 256, A.mult, A.add)))
+        o_col.append(mark(vec.memset(T.ee[:], 0.0)))
+
+    if r < 2:
+        m_w0 = mark(vec.memset(T.w0[:], 0))
     else:
-        send(own[:], own[:], [h for h in JOIN if r in JOIN[h][0:2]], "arrl%d" % r)
-    if near:
-        send(T.litb[:], T.lland[r], near, "arrk%d" % r)
-        send(own[:], own[:], near, "arrl%d" % r)
+        join_columns()
+    wait("a", m_one)
+    m_zf = mark(act.activation(T.zf[0:8, :], T.one[0:8, 0:64], F.Copy, scale=0.0))
+    m_ch = mark(act.activation(T.chalf[0:1, :], T.one[0:1, 0:128], F.Copy, scale=-3.5))
+    count(act.activation(T.thr[0:64, 18:BW], T.one[0:64, 0:18], F.Copy, scale=-1024.0), "thr")
+    count(act.activation(T.thr[64:128, 0:18], T.one[64:128, 0:18], F.Copy, scale=-1024.0), "thr")
+    wait("a", c_rr)
+    m_kr = mark(act.activation(T.krow[0:1, 0:BW], T.rr[0:1, 0:BW], F.Identity, bias=128.0))
+    count(act.activation(T.thr[0:64, 0:18], T.rr[0:64, 0:18], F.Copy), "thr")
+    m_th = count(act.activation(T.thr[64:128, 18:BW], T.rr[64:128, 18:BW], F.Copy), "thr")
+    wait("a", c_sel)
+    m_sn = mark(act.activation(T.seln[0:8, :], T.sel[0:8, :], F.Copy, scale=-1.0))
+    wait("a", o_seed, o_rep, o_rs)
+    a_mw0 = mark(act.activation(T.mw[:, 0:UW], T.seed[:].indirect(T.rep[:]), F.Copy))
+    c_rl = mark(act.activation(T.rl[:], T.rlh[:].indirect(T.rep[:, 0:10]), F.Copy))
+    wait("a", a_mw0)
+    for n in range(1, 5):
+        count(act.activation(T.mw[:, UW * n:UW * n + UW], T.mw[:, 0:UW], F.Copy), "mw")
 
-    if helper:
-        wait("v", o_p15)
-        o_pm0 = mark(vec.tensor_scalar(T.pm0[:, 0:1], T.p15[:, 0:1], 0.0, None, A.is_equal))
-        o_pm1 = mark(vec.tensor_scalar(T.pm1[:, 0:1], T.p15[:, 0:1], 1.0, 32.0, A.is_equal, A.mult))
-        m_cw = mark(vec.memset(T.cw[:, S:S + Q], 0.0))
-    for k in range(len(stages)):
-        if k not in m_w:
-            zero_window(k)
-    if helper:
-        wait("v", c_d15, c_d14, o_pm0, o_pm1)
-        o_e15 = mark(vec.tensor_scalar(T.e15[:], T.d15[:], T.pm0[:, 0:1], None, A.mult))
-        o_e14 = mark(vec.tensor_scalar(T.e14[:], T.d14[:], T.pm1[:, 0:1], None, A.mult))
-        wait("v", o_e15, o_e14)
-        o_ee = mark(vec.tensor_tensor(T.ee[:], T.e15[:], T.e14[:], A.add))
-        wait("a", c_hib, o_h5)
-        a_hi = mark(act.activation(T.hi[:], T.hib[:], F.Identity, bias=T.h5[:, 0:1]))
-        wait("a", o_h80, m_one)
-        a_hix = mark(act.activation(T.hix[:], T.one[:, 0:32], F.Identity, scale=T.h80[:, 0:1]))
-        wait("s", m_id0, m_id1, c_lo)
-        syn.dma_start(T.idw[0:128:16, :], T.lo[:]).then_inc(T.sem.d_id, 16)
-        wait("s", a_hi)
-        syn.dma_start(T.idw[1:128:16, :], T.hi[:]).then_inc(T.sem.d_id, 16)
-        wait("s", m_cw)
-        syn.dma_start(T.cw[0:128:16, S:S + Q], T.lo[:, 0:32]).then_inc(T.sem.d_cw, 16)
-        wait("s", a_hix)
-        syn.dma_start(T.cw[1:128:16, S:S + Q], T.hix[:]).then_inc(T.sem.d_cw, 16)
+    wait("g", d_stg)
+    send([(d, T.stg[d], T.land[r]) for d in others(r)], shares(r, others(r)), lit_sem(r))
 
-    for k in range(len(stages)):
-        for n, v in enumerate(stages[k]):
-            at = base[k] + Q * n
-            dst = wins[k][0:128:16, at:at + Q]
-            wait("s", m_w[k])
-            if v == r:
-                wait("s", o_lb)
-                syn.dma_start(dst, T.litb[:]).then_inc(T.sem["lit%d" % v], 16)
-            else:
-                wait("s", arrived("arrk%d" % v, v))
-                syn.dma_start(dst, T.lland[v]).then_inc(T.sem["lit%d" % v], 16)
+    wait("v", d_ln, m_zf, m_t0)
+    o_t = mark(vec.tensor_tensor_scan(xs(XT, 1, 64), T.lni[0:8, 0:63], T.zf[0:8, 0:63], -64.0, A.add, A.add))
+    wait("v", d_fr)
+    o_xf = mark(vec.tensor_scalar(xs(XF), T.fri[0:8, :], -1280.0, None, A.add))
+    wait("v", o_t)
+    o_xm = mark(vec.tensor_scalar(xs(XM), xs(XT), BIG128, -BIG128, A.add, A.add))
+    wait("v", o_xf, m_e0)
+    o_xe = mark(vec.tensor_tensor(xs(XE, 1, 64), xs(XF, 0, 63), T.lni[0:8, 0:63], A.add))
+    wait("p", c_fine, m_one, m_ch)
+    pe.matmul(T.pwb[:, 0:1], T.fine[0:1, :], T.one[0:1, 0:1], True, False)
+    p_col = mark(pe.matmul(T.pwb[:, 0:1], T.chalf[0:1, :], T.one[0:1, 0:1], False, True))
 
-    if helper:
-        v0, v1, c0, nc, buf, sem, calls = JOIN[r]
-        l0, l1 = T["ls%d" % v0], T["ls%d" % v1]
-        half = nc // 2
-        for q in ("v", "a"):
-            wait(q, ("d_id", 32), arrived("arrl%d" % v0, v0))
-        i_v = mark(vec.tensor_copy(T.cw[:, 0:HALF], T.idw[:].indirect(l0[:, 0:64])))
-        i_a = mark(act.activation(T.cw[:, HALF:S], T.idw[:].indirect(l0[:, 64:128]), F.Copy))
-        for q in ("v", "a"):
-            wait(q, i_v, i_a, ("d_cw", 32), arrived("arrl%d" % v1, v1))
-        j_v = mark(vec.tensor_copy(T.cr[:, 0:16 * half], T.cw[:].indirect(l1[:, c0:c0 + half])))
-        j_a = mark(act.activation(T.cr[:, 16 * half:16 * nc], T.cw[:].indirect(l1[:, c0 + half:c0 + nc]), F.Copy))
-        wait("p", o_ee, j_v, j_a)
-        for q in range(16):
-            last = pe.matmul(T.pjn[:, 0:nc], T.ee[:, 15 - q:143 - q], T.cr[:, q:16 * nc:16], q == 0, q == 15)
-        p_jn = mark(last)
-        wait("v", p_jn)
-        o_jn = mark(vec.tensor_copy(T[buf][:], T.pjn[:, 0:nc]))
-        wait("g", o_jn)
-        for c in calls:
-            send(T[buf][:], T[buf][:], c, sem)
+    wait("p", m_kr)
+    for b in range(4):
+        pe.matmul(T["po%d" % b][:, 0:BW], T.one[0:1, 0:128], T.krow[0:1, 0:BW], True, False)
 
-    prev = []
-    for k, st in enumerate(stages):
-        v = st[-1]
-        win = wins[k][:, 0:base[k] + Q * len(st)]
-        out = T.yo if k == len(stages) - 1 else wins[k + 1]
-        if len(st) == 1:
-            lst = T["ls%d" % v]
-            lists = (lst[:, 0:64], lst[:, 64:128])
-            got = [o_ls if v == r else arrived("arrl%d" % v, v)] * 2
-        elif v == 5:
-            lists = (T.ca[:], T.cb[:])
-            got = [arrived("arrc0", 2), arrived("arrc1", 3)]
+    def turn(col, k, sel, start, stop):
+        ps = T.pq[:, 4 * col:4 * col + 4]
+        pe.matmul(ps, T.xx[0:8, 64 + 128 * k:192 + 128 * k], sel[0:8, 0:8:2], start, False)
+        return pe.matmul(ps, T.xx[0:8, 128 * k:128 + 128 * k], sel[0:8, 1:8:2], False, stop)
+
+    single = r == 0
+    wait("p", c_sel, m_sn, m_xx, o_t, m_t0)
+    turn(XT, XT, T.sel, True, True)
+    if not single:
+        wait("p", o_xf)
+        turn(XF, XF, T.sel, True, True)
+    wait("p", o_xm)
+    turn(XM, XM, T.sel, True, True)
+    if single:
+        wait("p", o_xf)
+        turn(XF, XF, T.sel, True, False)
+    wait("p", o_xe, m_e0)
+    p_k = mark(turn(XF if single else XE, XE, T.seln, not single, True))
+
+    if r >= 2:
+        m_w0 = mark(vec.memset(T.w0[:], 0))
+    else:
+        join_columns()
+    wait("v", p_col)
+
+    wait("s", d_own, ("arrk0", lit_in([0])), ("arrka", lit_in([1, 2, 3])))
+    d_lt0 = count(syn.dma_start(T.lt0[:], T.land[0:4]), "d_lt0", 16)
+    for q, hs in (("a", range(4, 8)), ("s", range(0, 4))):
+        wait(q, m_w0, d_own if r == 0 else ("arrk0", lit_in([0])))
+        for h in hs:
+            d_w0 = count(queues[q].dma_start(T.w0[16 * h:16 * h + 1, :], T.land[0]), "d_w0", 16)
+    wait("s", ("arrkb", lit_in([4, 5, 6, 7])))
+    d_lt1 = count(syn.dma_start(T.lt1[:], T.land[4:8]), "d_lt1", 16)
+
+    wait("v", p_k, m_th)
+    p_out, o_snd = {}, []
+
+    def factors(b):
+        cols = slice(BW * b, BW * b + BW)
+        now, old = slice(BW * b + 1, BW * b + BW), slice(BW * b, BW * b + BW - 1)
+        xf, xe, st, sk = [T.pq[:, 4 * k + b:4 * k + b + 1] for k in (XF, XE, XT, XM)]
+        lp, lm = T.lp[:, 128 * b:128 * b + 128], T.lm[:, 128 * b:128 * b + 128]
+        name = "f%d" % b
+        count(vec.tensor_scalar(T.bf[:, cols], T.thr[:, 0:BW], sk, xf, A.is_ge, A.mult), name)
+        count(vec.tensor_scalar(lp, T.fine[:], sk, st, A.add, A.is_ge), name)
+        if single:
+            made = count(vec.tensor_scalar(T.be[:, cols], T.thr[:, 0:BW], sk, xf, A.is_equal, A.mult), name)
+            prods = [(T.one[:, 0:128], T.bf[:, old]), (lp, T.be[:, now])]
         else:
-            lists = (T.cf[:, 0:64], T.cf[:, 64:128])
-            got = [arrived("arrc2", 1)] * 2
-        lits = [("lit%d" % x, 16) for x in st]
-        wait("v", *lits, got[0], *prev)
-        wait("a", *lits, got[1], *prev)
-        prev = [mark(vec.tensor_copy(out[:, 0:HALF], win.indirect(lists[0]))),
-                mark(act.activation(out[:, HALF:S], win.indirect(lists[1]), F.Copy))]
-    wait("s", prev[0])
-    syn.dma_start(T.y[:, 0:HALF], T.yo[0:128:16, 0:HALF]).then_inc(T.sem.d_y0, 16)
-    wait("a", prev[1])
-    act.dma_start(T.y[:, HALF:S], T.yo[0:128:16, HALF:S]).then_inc(T.sem.d_y1, 16)
-    wait("g", ("loc", sent[0]))
-    wait("s", ("d_y0", 16))
-    wait("a", ("d_y1", 16))
-    for name in marks:
-        if name not in waited:
-            wait("s", (name, 1))
+            count(vec.tensor_scalar(T.be[:, cols], T.thr[:, 0:BW], sk, xe, A.is_ge, A.mult), name)
+            made = count(vec.tensor_scalar(lm, T.fine[:], sk, st, A.add, A.is_lt), name)
+            prods = [(lm, T.bf[:, old]), (lm, T.be[:, old]), (lp, T.bf[:, now]), (lp, T.be[:, now])]
+        wait("p", made)
+        for k, (left, right) in enumerate(prods):
+            last = pe.matmul(T["po%d" % b][:, 0:BW - 1], left, right, False, k == len(prods) - 1)
+        p_out[b] = mark(last)
+
+    def as_list(out, b, a, n):
+        return mark(vec.tensor_scalar(out, T["po%d" % b][:, a:a + n], T.pwb[:, 0:1], 67.5, A.add, A.add))
+
+    def hand_out(b, calls):
+        wait("v", p_out[b])
+        o_snd.append(as_list(T.snd[:, 40 * b:40 * b + 34], b, 0, 34))
+        wait("g", o_snd[-1])
+        for dests in calls:
+            at = {d: 40 * b + 18 * (mine.index(d) % 2) for d in dests}
+            send([(d, T.snd[:, at[d]:at[d] + 16], T.lst[:, 16 * r:16 * r + 16]) for d in dests],
+                 shares(r, dests), list_sem(r))
+
+    plan = pairs(r)
+    for n in range(6):
+        if n < 4:
+            factors(plan[n][0])
+        if n >= 2:
+            hand_out(*plan[n - 2])
+    o_own = as_list(T.lst[:, 16 * r:16 * r + 16], mine.index(r) // 2, 18 * (mine.index(r) % 2), 16)
+    if r < 2:
+        c_fr = first_row()
+
+    wait("v", a_mw0, *o_col)
+    for n in range(5, MW // UW):
+        o_mw = count(vec.tensor_copy(T.mw[:, UW * n:UW * n + UW], T.mw[:, 0:UW]), "mw")
+    c_id = mark(vec.tensor_scalar(T.ident[:], T.fine[:], -3.5, T.pwb[:, 0:1], A.add, A.is_equal))
+    c_ee = mark(vec.tensor_copy(T.ee[:, 15:144:16], T.rlh[:, 0:9]))
+    for at in (128, 288):
+        count(vec.tensor_scalar(T.jw[:, at:at + 16], T.fine[:, 0:16], 2.0, ja, A.mult, A.add), "js")
+        c_js = count(vec.tensor_scalar(T.jw[:, at + 16:at + 32], T.fine[:, 0:16], 2.0, jb, A.mult, A.add), "js")
+    wait("v", c_fr)
+    for n in range(8):
+        c_pick = count(vec.tensor_scalar(T.pick[:, 128 * n:128 * n + 128], T.frow[:], 2.0 * n, pc, A.add, A.is_equal), "pick")
+
+    def twice(hf, dma):
+        wait("v", dma)
+        for n in range(2):
+            made = count(vec.tensor_copy(T.lrep[:, 32 * hf + 16 * n:32 * hf + 16 * n + 16], T["lt%d" % hf][:]), "lr%d" % hf)
+        return made
+
+    def got(v):
+        if v >= 2:
+            return [("arrl", list_in(range(2, NV))), o_own]
+        return [o_own] if v == r else [(list_sem(v), list_in([v]))]
+
+    done = {}
+    made = {}
+    ybanks, order = [T.po0, T.po1, T.po2], []
+    wait("p", o_own, *o_snd, c_id, c_rl)
+
+    def mask(x, a, b):
+        wait("a", o_mw, *(got(x) if x < NV else [done["lst%d" % x]]))
+        return mark(act.activation(T.msk[:, 256 * x + 16 * a:256 * x + 16 * b],
+                                   T.mw[:].indirect(T.lst[:, 16 * x + a:16 * x + b]), F.Copy))
+
+    def lows(a, b):
+        wait("v", *got(a))
+        return mark(vec.tensor_scalar(T.low[:, 16 * a:16 * b], T.lst[:, 16 * a:16 * b], -7.5, 0.0625, A.add, A.mult))
+
+    def gather(out, win, x, a, b):
+        halves = done["m%d" % x]
+        wait("v", done["low%d" % x], *(halves if b - a == 16 else halves[-1:] if a == 0 else halves[0:1]))
+        return vec.tensor_tensor(out[:, 16 * a:16 * b], win.indirect(T.low[:, 16 * x + a:16 * x + b]),
+                                 T.msk[:, 256 * x + 16 * a:256 * x + 16 * b], A.mult)
+
+    def version(v, x, w, a, b):
+        out = T.res[:, 256 * v:256 * v + 256]
+        if v == 0:
+            wait("v", d_w0, *got(0))
+            return vec.tensor_copy(out[:, 16 * a:16 * b], T.w0[:].indirect(T.lst[:, a:b]))
+        wait("v", *made[w])
+        return gather(out, T.win[:, WIN[w][0]:WIN[w][0] + WIN[w][1]], x, a, b)
+
+    def rows(v, *deps):
+        py = ybanks[len(order) % 3]
+        wait("p", *deps, done["y%d" % order[-3]] if len(order) >= 3 else None)
+        order.append(v)
+        pe.matmul(py[:, 0:8], T.res[:, 256 * v:256 * v + 256:2], T.rl[:, 0:8], True, True)
+        done["p%d" % v] = mark(pe.matmul(py[:, 8:16], T.res[:, 256 * v + 1:256 * v + 256:2], T.rl[:, 0:8], True, True))
+
+    def hand_on(v, q="v"):
+        yo, src = T.yo[:, 16 * v:16 * v + 16], ybanks[order.index(v) % 3][:, 0:16]
+        wait(q, done["p%d" % v])
+        done["y%d" % v] = mark(vec.tensor_copy(yo, src) if q == "v" else act.activation(yo, src, F.Copy))
+        if v == r:
+            wait("s", done["y%d" % v])
+            count(syn.dma_start(T.y[r], yo), "d_y", 16)
+            call = [c for c in CALLS if r in c][0]
+            wait("s", ("arry", sum(len(shares(x, [d for d in call if d != x])[r]) for x in others(r))))
+            for a, b in ((0, r), (r + 1, NV)):
+                if a < b:
+                    count(syn.dma_start(T.y[a:b], T.yl[a:b]), "d_y", 16)
+        for call in CALLS:
+            dests = [d for d in call if d != r]
+            if v == call[-1] and dests:
+                wait("g", *[done["y%d" % d] for d in dests])
+                send([(d, T.yo[:, 16 * d:16 * d + 16], T.yl[r]) for d in dests], shares(r, dests), "arry")
+
+    def join(n, name):
+        a, b = {"": (0, 16), "a": (8, 16), "b": (0, 8)}[name[2:]]
+        out = T.rj[:, 256 * n:256 * n + 256]
+        wait("v", done["jw%d" % n], c_js)
+        done[name] = mark(gather(out, T.jw[:, 160 * n:160 * n + 160], J + 1 + 2 * n, a, b))
+        if a == 0:
+            later.append(lambda: back(n, name))
+
+    def back(n, name):
+        wait("p", c_ee, done.get(name[0:2] + "a"), done[name])
+        for u in range(16):
+            last = pe.matmul((T.pj, T.pq)[n][:, 0:16], T.ee[:, 15 - u:143 - u], T.rj[:, 256 * n + u:256 * n + 256:16], u == 0, u == 15)
+        done["back%d" % n] = mark(last)
+
+    def list_window():
+        wait("p", c_pick, done["lf"])
+        for n in range(8):
+            last = pe.matmul(T.po3[:, n:384:8], T.pick[:, 128 * n:128 * n + 128], T.lf[:], True, True)
+        done["pjw"] = mark(last)
+
+    later = []
+
+    def on_vector(name):
+        if name == "low1":
+            done[name] = lows(1, 2)
+        elif name == "lows":
+            o = lows(2, NV)
+            for x in range(2, NV):
+                done["low%d" % x] = o
+        elif name == "lf":
+            wait("v", *got(J))
+            done[name] = mark(vec.tensor_scalar(T.lf[:], T.lst[:, 16 * J:16 * J + 48], -1024.0, None, A.add))
+            later.append(list_window)
+        elif name[0:3] == "lit":
+            done[name] = twice(int(name[3]), (d_lt0, d_lt1)[int(name[3])])
+        elif name[0] == "y":
+            hand_on(int(name[1]))
+        elif name[0] == "j":
+            join(int(name[1]), name)
+        elif name[0] == "c":
+            n = int(name[1])
+            x, src = NV + n, (T.pj, T.pq)[n][:, 0:16]
+            wait("v", done["back%d" % n])
+            done["lst%d" % x] = mark(vec.tensor_scalar(T.lst[:, 16 * x:16 * x + 16], src, 1024.0, None, A.add))
+            done["low%d" % x] = mark(vec.tensor_scalar(T.low[:, 16 * x:16 * x + 16], src, 1016.5, 0.0625, A.add, A.mult))
+        else:
+            v = int(name[1])
+            a, b = {"a": (8, 16), "b": (0, 8), name[1]: (0, 16)}[name[-1]]
+            done[name] = mark(version(v, v, v, a, b))
+            if name[-1] != "a":
+                rows(v, done[name], done.get(name[0:2] + "a"))
+
+    def on_scalar(name):
+        if name[0] == "Y":
+            hand_on(int(name[1]), "a")
+        elif name[0] == "j":
+            n = int(name[2])
+            wait("a", done["pjw"])
+            done[name] = mark(act.activation(T.jw[:, 160 * n:160 * n + 128], T.po3[:, 256 * n:256 * n + 128], F.Copy))
+        else:
+            x = int(name[1:])
+            done[name] = [mask(x, 8, 16), mask(x, 0, 8)] if x in HALVES else [mask(x, 0, 16)]
+
+    for name in VFIRST:
+        on_vector(name)
+    while later:
+        later.pop(0)()
+    for name in AFIRST:
+        on_scalar(name)
+    c_a = c_b = None
+    for k, (v, x, w, nxt) in enumerate(CHAIN):
+        res = 256 * v
+        if nxt is None:
+            rows(v, mark(version(v, x, w, 0, 16)))
+            hand_on(v)
+            break
+        g_1 = count(version(v, x, w, 8, 16), "g1")
+        g_2 = count(version(v, x, w, 0, 8), "g2")
+        at, n = WIN[nxt][0], WIN[nxt][1] - 128
+        wait("p", c_a)
+        for u in range(nxt, nxt + n // 32):
+            wait("p", done["lit%d" % (u // 4)])
+            for a in range(0, 128, 32):
+                pe.matmul(T.pwa[a:a + 32, 64 + 32 * (u - nxt):96 + 32 * (u - nxt)], T.lrep[:, 32 * (u // 4):32 * (u // 4) + 32],
+                          T.ident[:, 32 * (u % 4):32 * (u % 4) + 32], True, True)
+        wait("p", g_1)
+        pe.matmul(T.pwa[:, 0:64], T.rl[:, 0:128], T.res[:, res + 128:res + 256:2], True, False)
+        p_a = count(pe.matmul(T.pwa[:, 0:64], T.rl[:, 8:136], T.res[:, res + 129:res + 256:2], False, True), "pa")
+        wait("p", g_2, c_b)
+        pe.matmul(T.pwb[:, 0:64], T.rl[:, 0:128], T.res[:, res:res + 128:2], True, False)
+        p_b = count(pe.matmul(T.pwb[:, 0:64], T.rl[:, 8:136], T.res[:, res + 1:res + 128:2], False, True), "pb")
+        rows(v)
+        wait("a", p_a)
+        c_a = count(act.activation(T.win[:, at + 64:at + 128 + n], T.pwa[:, 0:64 + n], F.Copy), "ca")
+        cut = VSLOT[k].index("|")
+        for name in VSLOT[k][:cut]:
+            on_vector(name)
+        wait("v", p_b)
+        c_b = count(vec.tensor_copy(T.win[:, at:at + 64], T.pwb[:, 0:64]), "cb")
+        made[nxt] = [c_a, c_b]
+        for name in VSLOT[k][cut + 1:]:
+            on_vector(name)
+        while later:
+            later.pop(0)()
+        for name in ASLOT[k]:
+            on_scalar(name)
+    wait("g", ("loc", total["loc"]))
+    for name in total:
+        if waited.get(name, 0) < total[name]:
+            wait("s", (name, total[name]))

@@ -7,16 +7,37 @@ Q = 512
 BW = 36
 UW = 384
 MW = S + 2 * Q
+AT = {x: 16 * n for n, x in enumerate((0, 4, 1, 2, 6, 7, 3, 5, 8, 9))}
+YBANKS = ["po0", "po1", "po2", "pq", "pj", "po0", "po3", "pwb"]
+OFF = (1024.0, 1024.0)
+EARLIER = (3, 5)
+LATER = (4, 6)
+FROM = {3: (3, 3), 5: (5, 5), 7: (7, 7)}
 J = 3
 BIG128 = float(3 * 2 ** 29)
 BIG32 = float(3 * 2 ** 27)
 WIN = {1: (0, 160), 2: (160, 160), 3: (320, 192), 5: (512, 192), 7: (704, 160)}
-CHAIN = [(0, 0, 0, 1), (1, 1, 1, 2), (2, 2, 2, 3), (4, 8, 3, 5), (6, 9, 5, 7), (7, 7, 7, None)]
+CHAIN = [(0, 0, 0, 1), (1, 1, 1, 2), (2, 2, 2, 3), (4, 8, 3, 5), (6, 9, 5, 7)]
 HALVES = (8, 9)
+NA, NB = 3, 3
+LTFIRST = True
+WHOLE = ()
 CALLS = [[v] for v in range(NV)]
-VFIRST, AFIRST = ["lf", "low1", "lows", "lit0"], ["m4", "jw0", "jw1", "m1"]
-VSLOT = [["j0", "|", "lit1"], ["j1", "|", "c0"], ["y0", "y1", "c1", "|", "y2"], ["v3", "|"], ["v5", "|"]]
-ASLOT = [["m6", "m2"], ["m3", "m8"], ["m9"], ["m5", "m7", "Y4", "Y3"], ["Y6", "Y5"]]
+ORDER = [[2, 1, 3, 0] if v in (3, 4) else [0, 1, 2, 3] for v in range(NV)]
+LAG = 2
+REP = 2
+LMA = ()
+LITFIRST = ()
+EARLY = [4] + [2] * 7
+KIND = [3, 1, 0, 0, 0, 0, 0, 2]
+VS = "lf1 j0 low1267 | u3 / j1 | c0 / u5 y0 c1 | lit1 / v3 | y4 / v5 | y6 / v7 Y5 y7"
+V0 = "lf0 j1 low412 | u5 / j0 | u3 / c1 c0 low7 y0 | lit1 / v3 | y4 / v5 | y6 / v7 Y5 y7"
+AS = "m6 jw1 m2 / m3 m8 / m9 Y1 Y2 / m5 Y3 m7 / "
+A0 = "m4 jw0 m2 / m5 m3 / m8 Y1 m9 / Y2 Y3 m7 / "
+PLAN = [("lf0 mwl lit0 low4", "js0 js1 m4 jw0 m1", VS, AS),
+        ("mwl lf1 low6 lit0", "js0 js1 m6 jw1 m1", V0, A0),
+        ("mwl lit0 lf0 low4", "js0 js1 m4 jw0 m1", VS, AS),
+        ("mwl lf1 low6", "js0 js1 m6 jw1 m1", V0, A0)]
 
 SCRATCH = {
     "lni": ("sbuf", [128, 64], "int32"),
@@ -34,13 +55,15 @@ SCRATCH = {
     "seed": ("sbuf", [128, 16], "bfloat16"),
     "cc": ("sbuf", [128, UW // 16], "bfloat16"),
     "cols": ("sbuf", [128, 8], "float32"),
+    "colb": ("sbuf", [128, 16], "bfloat16"),
     "lp": ("sbuf", [128, 512], "bfloat16"),
     "lm": ("sbuf", [128, 512], "bfloat16"),
     "bf": ("sbuf", [128, 4 * BW], "float16"),
     "be": ("sbuf", [128, 4 * BW], "float16"),
     "snd": ("sbuf", [128, 4 * 40], "uint16"),
-    "lst": ("sbuf", [128, 160], "uint16"),
-    "low": ("sbuf", [128, 160], "uint16"),
+    "sndf": ("sbuf", [128, 4 * 40], "float16"),
+    "lst": ("sbuf", [128, 176], "uint16"),
+    "low": ("sbuf", [128, 176], "uint16"),
     "rep": ("sbuf", [128, UW // 16], "uint16"),
     "mw": ("sbuf", [128, MW], "bfloat16"),
     "ident": ("sbuf", [128, 128], "bfloat16"),
@@ -51,17 +74,19 @@ SCRATCH = {
     "lt1": ("sbuf", [128, 16], "int32"),
     "lrep": ("sbuf", [128, 64], "bfloat16"),
     "win": ("sbuf", [128, 864], "bfloat16"),
-    "msk": ("sbuf", [128, 10 * 256], "bfloat16"),
+    "msk": ("sbuf", [128, 11 * 256], "bfloat16"),
     "res": ("sbuf", [128, NV * 256], "bfloat16"),
     "yo": ("sbuf", [128, NV * 16], "float32"),
     "frow": ("sbuf", [128, 128], "bfloat16"),
     "pick": ("sbuf", [128, 1024], "bfloat16"),
     "ee": ("sbuf", [128, 144], "bfloat16"),
+    "eh": ("sbuf", [128, 16], "bfloat16"),
     "lf": ("sbuf", [128, 48], "float16"),
-    "jw": ("sbuf", [128, 320], "float32"),
-    "rj": ("sbuf", [128, 512], "float16"),
+    "jw": ("sbuf", [128, 480], "float32"),
+    "rj": ("sbuf", [128, 768], "float16"),
     "stg": ("dram", [NV, 128, 4], "int32"),
     "land": ("dram", [NV, 128, 4], "int32"),
+    "first": ("dram", [REP, 128, 4], "int32"),
     "yl": ("dram", [NV, 128, 16], "float32"),
     "pq": ("psum", [128, 512], "float32"),
     "po0": ("psum", [128, 512], "float32"),
@@ -73,10 +98,10 @@ SCRATCH = {
     "pwb": ("psum", [128, 512], "float32"),
 }
 
-NOPS = 110
+NOPS = 104
 SEMAPHORES = (["d_ln", "d_fr", "d_stg", "d_own", "d_w0", "d_lt0", "d_lt1", "d_y", "loc", "arrk0", "arrka", "arrkb",
-               "arrl0", "arrl1", "arrl", "arry", "g1", "g2", "pa", "pb", "ca", "cb", "mw", "lr0", "lr1", "sel", "thr",
-               "pick", "js", "f0", "f1", "f2", "f3"] + ["op%d" % k for k in range(NOPS)])
+               "arrl0", "arrl1", "arrl2", "arrl3", "arrl4", "arrl5", "arrl6", "arrl7", "arry",
+               "g1", "g2", "pa", "pb", "ca", "cb", "mw", "lr0", "lr1", "sel", "thr", "pick", "js0", "w0", "iss", "f0", "f1", "f2", "f3"] + ["op%d" % k for k in range(NOPS)])
 
 
 def rank_program(g, core, T, topo):
@@ -126,13 +151,13 @@ def rank_program(g, core, T, topo):
         return [d for d in range(NV) if d != src]
 
     def docs(src):
-        return list(range(NV)) if src >= 2 else others(src) + [src]
+        return others(src) + [src]
 
     def pairs(src):
         out = []
-        for b in range(4):
+        for b in ORDER[src]:
             two = docs(src)[2 * b:2 * b + 2]
-            calls = [two[0:1], two[1:2]] if b == 3 else [two]
+            calls = [two[0:1], two[1:2]] if NV - 1 in two else [two]
             calls = [[d for d in c if d != src] for c in calls]
             out.append((b, [c for c in calls if c]))
         return out
@@ -141,22 +166,30 @@ def rank_program(g, core, T, topo):
         tr = []
         for d, src, dst in pieces:
             rid, pid, _se = topo.addr(T.cores[d])
-            tr.append(RemoteDMATransfer(dst_ids=[DstId(rid=rid, pnc=pid)], dma_engine_mask=sum(1 << e for e in engines[d]),
-                                        remote_sem=T.sem[sem], srcs=[src], dsts=[dst]))
+            dsts = dst if isinstance(dst, list) else [dst]
+            tr.append(RemoteDMATransfer(dst_ids=[DstId(rid=rid, pnc=pid)] * len(dsts),
+                                        dma_engine_mask=sum(1 << e for e in engines[d]),
+                                        remote_sem=T.sem[sem], srcs=[src], dsts=dsts))
             total["loc"] = total.get("loc", 0) + len(engines[d])
         g.remote_dma_fused(tr, local_sem=T.sem.loc)
 
+    def lit_calls(src):
+        return [others(src)]
+
+    def lit_share(src, dests):
+        return shares(src, dests)
+
     def lit_in(vs):
-        return sum(len(shares(v, others(v))[r]) for v in vs if v != r)
+        return sum(len(shares(v, others(v))[r]) * (REP if v == 0 else 1) for v in vs if v != r)
 
     def list_in(vs):
         return sum(len(shares(v, c)[r]) for v in vs if v != r for _b, calls in pairs(v) for c in calls if r in c)
 
     def lit_sem(v):
-        return "arrk0" if v == 0 else "arrka" if v < 4 else "arrkb"
+        return "arrk0" if v == 0 else "arrka" if v <= 4 else "arrkb"
 
     def list_sem(v):
-        return "arrl0" if v == 0 else "arrl1" if v == 1 else "arrl"
+        return "arrl%d" % v
 
     d_stg = count(syn.dma_start(T.stg[:], T.lit[:]), "d_stg", 16)
     d_ln = count(act.dma_start(T.lni[0:8, :], T.ln[:]), "d_ln", 16)
@@ -178,12 +211,6 @@ def rank_program(g, core, T, topo):
     cuts = [i for i in range(NV) if i == 0 or mine[i] != mine[i - 1] + 1] + [NV]
     for a, b in zip(cuts, cuts[1:]):
         c_sel = count(g.affine_select(T.sel[0:8, a:b], T.one[0:8, a:b], [[-1, b - a]], A.is_equal, 0.0, -mine[a], 1), "sel")
-
-    def first_row():
-        return mark(g.iota(T.frow[:], [[0, 8], [1, 2], [16, 8]], 0, 0, **imp))
-
-    if r >= 2:
-        c_fr = first_row()
     m_c0 = mark(vec.memset(T.cc[:], 16.0))
     m_xx = mark(vec.memset(T.xx[0:8, :], 0.0))
     wait("v", c_z)
@@ -198,18 +225,7 @@ def rank_program(g, core, T, topo):
     wait("v", o_u)
     o_seed = mark(vec.tensor_scalar(T.seed[:], T.fine[:, 0:16], 0.25, uc, A.mult, A.is_equal))
     o_rep = mark(vec.tensor_scalar(T.rep[:], T.cc[:], uc, 0.5, A.add, A.mult))
-    o_col = []
-
-    def join_columns():
-        o_col.append(mark(vec.tensor_scalar(pc, zc, 271.0, 0.5, A.add, A.mult)))
-        o_col.append(mark(vec.tensor_scalar(ja, uc, 0.5, 1672.0, A.mult, A.add)))
-        o_col.append(mark(vec.tensor_scalar(jb, uc, 0.5, 1672.0 + 256, A.mult, A.add)))
-        o_col.append(mark(vec.memset(T.ee[:], 0.0)))
-
-    if r < 2:
-        m_w0 = mark(vec.memset(T.w0[:], 0))
-    else:
-        join_columns()
+    count(vec.memset(T.w0[:, 0:Q // 2], 0), "w0")
     wait("a", m_one)
     m_zf = mark(act.activation(T.zf[0:8, :], T.one[0:8, 0:64], F.Copy, scale=0.0))
     m_ch = mark(act.activation(T.chalf[0:1, :], T.one[0:1, 0:128], F.Copy, scale=-3.5))
@@ -224,12 +240,11 @@ def rank_program(g, core, T, topo):
     wait("a", o_seed, o_rep, o_rs)
     a_mw0 = mark(act.activation(T.mw[:, 0:UW], T.seed[:].indirect(T.rep[:]), F.Copy))
     c_rl = mark(act.activation(T.rl[:], T.rlh[:].indirect(T.rep[:, 0:10]), F.Copy))
-    wait("a", a_mw0)
-    for n in range(1, 5):
-        count(act.activation(T.mw[:, UW * n:UW * n + UW], T.mw[:, 0:UW], F.Copy), "mw")
 
     wait("g", d_stg)
-    send([(d, T.stg[d], T.land[r]) for d in others(r)], shares(r, others(r)), lit_sem(r))
+    for dests in lit_calls(r):
+        send([(d, T.stg[d], [T.first[n] for n in range(REP)] if r == 0 else T.land[r]) for d in dests],
+             lit_share(r, dests), lit_sem(r))
 
     wait("v", d_ln, m_zf, m_t0)
     o_t = mark(vec.tensor_tensor_scan(xs(XT, 1, 64), T.lni[0:8, 0:63], T.zf[0:8, 0:63], -64.0, A.add, A.add))
@@ -254,89 +269,121 @@ def rank_program(g, core, T, topo):
 
     single = r == 0
     wait("p", c_sel, m_sn, m_xx, o_t, m_t0)
-    turn(XT, XT, T.sel, True, True)
+    turn(XT, XT, T.sel, True, False)
+    wait("p", o_xm)
+    turn(XT, XM, T.seln, False, True)
+    turn(XM, XM, T.sel, True, True)
     if not single:
         wait("p", o_xf)
         turn(XF, XF, T.sel, True, True)
-    wait("p", o_xm)
-    turn(XM, XM, T.sel, True, True)
     if single:
         wait("p", o_xf)
         turn(XF, XF, T.sel, True, False)
     wait("p", o_xe, m_e0)
     p_k = mark(turn(XF if single else XE, XE, T.seln, not single, True))
 
-    if r >= 2:
-        m_w0 = mark(vec.memset(T.w0[:], 0))
-    else:
-        join_columns()
+    m_w0 = count(vec.memset(T.w0[:, Q // 2:Q], 0), "w0")
     wait("v", p_col)
+    o_pb = mark(vec.tensor_copy(T.colb[:, 8:9], T.pwb[:, 0:1]))
+    o_col = [mark(vec.tensor_scalar(ja, uc, 0.5, 1672.0, A.mult, A.add)),
+             mark(vec.tensor_scalar(jb, uc, 0.5, 1672.0 + 256, A.mult, A.add))]
 
-    wait("s", d_own, ("arrk0", lit_in([0])), ("arrka", lit_in([1, 2, 3])))
-    d_lt0 = count(syn.dma_start(T.lt0[:], T.land[0:4]), "d_lt0", 16)
-    for q, hs in (("a", range(4, 8)), ("s", range(0, 4))):
-        wait(q, m_w0, d_own if r == 0 else ("arrk0", lit_in([0])))
-        for h in hs:
-            d_w0 = count(queues[q].dma_start(T.w0[16 * h:16 * h + 1, :], T.land[0]), "d_w0", 16)
-    wait("s", ("arrkb", lit_in([4, 5, 6, 7])))
+    def turned():
+        wait("s", d_own, ("arrka", lit_in([1, 2, 3, 4])))
+        return count(syn.dma_start(T.lt0[:], T.land[1:5]), "d_lt0", 16)
+
+    if LTFIRST and r > 0:
+        d_lt0 = turned()
+    wait("s", m_w0, d_own if r == 0 else ("arrk0", lit_in([0])))
+    n = 1 if r == 0 else REP
+    for h in range(0, 8, n):
+        d_w0 = count(syn.dma_start(T.w0[16 * h:16 * (h + n - 1) + 1:16, :], T.land[0] if r == 0 else T.first[:]), "d_w0", 16)
+    if EARLY[r] < 4:
+        syn.sem_inc(T.sem.iss, 1)
+    if not LTFIRST or r == 0:
+        d_lt0 = turned()
+    wait("s", ("arrkb", lit_in([5, 6, 7])))
     d_lt1 = count(syn.dma_start(T.lt1[:], T.land[4:8]), "d_lt1", 16)
 
     wait("v", p_k, m_th)
+    o_sr = mark(vec.tensor_copy(T.colb[:, 0:4], T.pq[:, 4 * XT:4 * XT + 4]))
     p_out, o_snd = {}, []
 
     def factors(b):
         cols = slice(BW * b, BW * b + BW)
         now, old = slice(BW * b + 1, BW * b + BW), slice(BW * b, BW * b + BW - 1)
-        xf, xe, st, sk = [T.pq[:, 4 * k + b:4 * k + b + 1] for k in (XF, XE, XT, XM)]
+        xf, xe, sk = [T.pq[:, 4 * k + b:4 * k + b + 1] for k in (XF, XE, XM)]
+        sr = T.colb[:, b:b + 1]
         lp, lm = T.lp[:, 128 * b:128 * b + 128], T.lm[:, 128 * b:128 * b + 128]
         name = "f%d" % b
         count(vec.tensor_scalar(T.bf[:, cols], T.thr[:, 0:BW], sk, xf, A.is_ge, A.mult), name)
-        count(vec.tensor_scalar(lp, T.fine[:], sk, st, A.add, A.is_ge), name)
         if single:
-            made = count(vec.tensor_scalar(T.be[:, cols], T.thr[:, 0:BW], sk, xf, A.is_equal, A.mult), name)
+            count(vec.tensor_scalar(T.be[:, cols], T.thr[:, 0:BW], sk, xf, A.is_equal, A.mult), name)
+            wait("v", o_sr)
+            made = count(vec.tensor_scalar(lp, T.fine[:], sr, None, A.is_ge), name)
             prods = [(T.one[:, 0:128], T.bf[:, old]), (lp, T.be[:, now])]
         else:
             count(vec.tensor_scalar(T.be[:, cols], T.thr[:, 0:BW], sk, xe, A.is_ge, A.mult), name)
-            made = count(vec.tensor_scalar(lm, T.fine[:], sk, st, A.add, A.is_lt), name)
-            prods = [(lm, T.bf[:, old]), (lm, T.be[:, old]), (lp, T.bf[:, now]), (lp, T.be[:, now])]
+            wait("v", o_sr)
+            made = count(vec.tensor_scalar(lp, T.fine[:], sr, None, A.is_ge), name)
+            if r in LMA:
+                wait("a", made)
+                more = mark(act.activation(lm, lp, F.Identity, bias=1.0, scale=-1.0))
+            else:
+                made = count(vec.tensor_scalar(lm, T.fine[:], sr, None, A.is_lt), name)
+            prods = [(lp, T.bf[:, now]), (lp, T.be[:, now]), (lm, T.bf[:, old]), (lm, T.be[:, old])]
         wait("p", made)
         for k, (left, right) in enumerate(prods):
+            if k == 2 and r in LMA:
+                wait("p", more)
             last = pe.matmul(T["po%d" % b][:, 0:BW - 1], left, right, False, k == len(prods) - 1)
         p_out[b] = mark(last)
 
     def as_list(out, b, a, n):
-        return mark(vec.tensor_scalar(out, T["po%d" % b][:, a:a + n], T.pwb[:, 0:1], 67.5, A.add, A.add))
+        return mark(vec.tensor_scalar(out, T["po%d" % b][:, a:a + n], T.pwb[:, 0:1], 67.5 - less, A.add, A.add))
+
+    early = r in EARLIER
+    less = OFF[EARLIER.index(r)] if early else 0.0
+    snd = T.sndf if early else T.snd
+    home = T.lf[:, 16 * EARLIER.index(r):16 * EARLIER.index(r) + 16] if early else T.lst[:, AT[r]:AT[r] + 16]
 
     def hand_out(b, calls):
         wait("v", p_out[b])
-        o_snd.append(as_list(T.snd[:, 40 * b:40 * b + 34], b, 0, 34))
+        o_snd.append(as_list(snd[:, 40 * b:40 * b + 34], b, 0, 34))
         wait("g", o_snd[-1])
         for dests in calls:
             at = {d: 40 * b + 18 * (mine.index(d) % 2) for d in dests}
-            send([(d, T.snd[:, at[d]:at[d] + 16], T.lst[:, 16 * r:16 * r + 16]) for d in dests],
-                 shares(r, dests), list_sem(r))
+            send([(d, snd[:, at[d]:at[d] + 16], home) for d in dests], shares(r, dests), list_sem(r))
 
     plan = pairs(r)
-    for n in range(6):
+    lag = 2 if single else LAG
+    for n in range(4 + lag):
         if n < 4:
             factors(plan[n][0])
-        if n >= 2:
-            hand_out(*plan[n - 2])
-    o_own = as_list(T.lst[:, 16 * r:16 * r + 16], mine.index(r) // 2, 18 * (mine.index(r) % 2), 16)
-    if r < 2:
-        c_fr = first_row()
+        if n - lag == EARLY[r]:
+            wait("g", ("iss", 1))
+        if n - lag == 3:
+            wait("v", a_mw0)
+            count(vec.tensor_copy(T.mw[:, 6 * UW:7 * UW], T.mw[:, 0:UW]), "mw")
+        if n >= lag:
+            hand_out(*plan[n - lag])
+    o_own = as_list(home, mine.index(r) // 2, 18 * (mine.index(r) % 2), 16)
 
-    wait("v", a_mw0, *o_col)
-    for n in range(5, MW // UW):
+    c_fr = mark(act.activation(T.frow[:], T.fine[:, 0:16].indirect(T.rep[:, 0:8]), F.Identity, bias=-59.5, scale=0.125))
+    wait("a", a_mw0)
+    for n in range(1, 1 + NA):
+        count(act.activation(T.mw[:, UW * n:UW * n + UW], T.mw[:, 0:UW], F.Copy), "mw")
+    wait("v", a_mw0, c_fr, o_pb)
+    for n in range(1 + NA, 6):
         o_mw = count(vec.tensor_copy(T.mw[:, UW * n:UW * n + UW], T.mw[:, 0:UW]), "mw")
-    c_id = mark(vec.tensor_scalar(T.ident[:], T.fine[:], -3.5, T.pwb[:, 0:1], A.add, A.is_equal))
-    c_ee = mark(vec.tensor_copy(T.ee[:, 15:144:16], T.rlh[:, 0:9]))
-    for at in (128, 288):
-        count(vec.tensor_scalar(T.jw[:, at:at + 16], T.fine[:, 0:16], 2.0, ja, A.mult, A.add), "js")
-        c_js = count(vec.tensor_scalar(T.jw[:, at + 16:at + 32], T.fine[:, 0:16], 2.0, jb, A.mult, A.add), "js")
-    wait("v", c_fr)
     for n in range(8):
-        c_pick = count(vec.tensor_scalar(T.pick[:, 128 * n:128 * n + 128], T.frow[:], 2.0 * n, pc, A.add, A.is_equal), "pick")
+        c_pick = count(vec.tensor_scalar(T.pick[:, 128 * n:128 * n + 128], T.frow[:], 16.0 * n, T.colb[:, 8:9],
+                                         A.add, A.is_equal), "pick")
+    c_id = mark(g.affine_select(T.ident[:], T.one[:], [[-1, 128]], A.is_equal, 0.0, 0, 1))
+    m_ee = mark(g.iota(T.ee[:], [[0, 144]], 0, 0, **imp))
+    c_e1 = mark(g.affine_select(T.eh[:, 0:9], T.one[:, 0:9], [[-16, 9]], A.is_ge, 0.0, 0, 1))
+    wait("g", m_ee, c_e1)
+    c_ee = mark(g.affine_select(T.ee[:, 15:144:16], T.eh[:, 0:9], [[16, 9]], A.is_ge, 0.0, 15, -1))
 
     def twice(hf, dma):
         wait("v", dma)
@@ -344,29 +391,32 @@ def rank_program(g, core, T, topo):
             made = count(vec.tensor_copy(T.lrep[:, 32 * hf + 16 * n:32 * hf + 16 * n + 16], T["lt%d" % hf][:]), "lr%d" % hf)
         return made
 
-    def got(v):
-        if v >= 2:
-            return [("arrl", list_in(range(2, NV))), o_own]
-        return [o_own] if v == r else [(list_sem(v), list_in([v]))]
+    def got(*vs):
+        return [o_own if v == r else (list_sem(v), list_in([v])) for v in vs]
 
     done = {}
     made = {}
-    ybanks, order = [T.po0, T.po1, T.po2], []
+    ybanks, jbanks = YBANKS, ["pj", "pq", "po3"][0:len(LATER)]
     wait("p", o_own, *o_snd, c_id, c_rl)
 
     def mask(x, a, b):
-        wait("a", o_mw, *(got(x) if x < NV else [done["lst%d" % x]]))
+        wait("a", o_mw, *(got(x) if x < NV else [done["mwl"]]), done["lst%d" % x] if x in EARLIER or x >= NV else None)
         return mark(act.activation(T.msk[:, 256 * x + 16 * a:256 * x + 16 * b],
-                                   T.mw[:].indirect(T.lst[:, 16 * x + a:16 * x + b]), F.Copy))
+                                   T.mw[:, 0:S + Q if x < NV else MW].indirect(T.lst[:, AT[x] + a:AT[x] + b]), F.Copy))
 
-    def lows(a, b):
-        wait("v", *got(a))
-        return mark(vec.tensor_scalar(T.low[:, 16 * a:16 * b], T.lst[:, 16 * a:16 * b], -7.5, 0.0625, A.add, A.mult))
+    def lows(xs):
+        wait("v", *got(*xs))
+        a, b = AT[xs[0]], AT[xs[-1]] + 16
+        return mark(vec.tensor_scalar(T.low[:, a:b], T.lst[:, a:b], -7.5, 0.0625, A.add, A.mult))
+
+    def whole(x, src, off):
+        done["lst%d" % x] = mark(vec.tensor_scalar(T.lst[:, AT[x]:AT[x] + 16], src, off, None, A.add))
+        done["low%d" % x] = mark(vec.tensor_scalar(T.low[:, AT[x]:AT[x] + 16], src, off - 7.5, 0.0625, A.add, A.mult))
 
     def gather(out, win, x, a, b):
         halves = done["m%d" % x]
         wait("v", done["low%d" % x], *(halves if b - a == 16 else halves[-1:] if a == 0 else halves[0:1]))
-        return vec.tensor_tensor(out[:, 16 * a:16 * b], win.indirect(T.low[:, 16 * x + a:16 * x + b]),
+        return vec.tensor_tensor(out[:, 16 * a:16 * b], win.indirect(T.low[:, AT[x] + a:AT[x] + b]),
                                  T.msk[:, 256 * x + 16 * a:256 * x + 16 * b], A.mult)
 
     def version(v, x, w, a, b):
@@ -378,19 +428,24 @@ def rank_program(g, core, T, topo):
         return gather(out, T.win[:, WIN[w][0]:WIN[w][0] + WIN[w][1]], x, a, b)
 
     def rows(v, *deps):
-        py = ybanks[len(order) % 3]
-        wait("p", *deps, done["y%d" % order[-3]] if len(order) >= 3 else None)
-        order.append(v)
+        py = ybanks[v]
+        wait("p", *deps, done["y0"] if v > 0 and py == ybanks[0] else None)
+        if py in jbanks:
+            x = NV + jbanks.index(py)
+            wait("p", done["lst%d" % x], done["low%d" % x])
+        py = T[py]
         pe.matmul(py[:, 0:8], T.res[:, 256 * v:256 * v + 256:2], T.rl[:, 0:8], True, True)
         done["p%d" % v] = mark(pe.matmul(py[:, 8:16], T.res[:, 256 * v + 1:256 * v + 256:2], T.rl[:, 0:8], True, True))
 
     def hand_on(v, q="v"):
-        yo, src = T.yo[:, 16 * v:16 * v + 16], ybanks[order.index(v) % 3][:, 0:16]
+        yo, src = T.yo[:, 16 * v:16 * v + 16], T[ybanks[v]][:, 0:16]
         wait(q, done["p%d" % v])
         done["y%d" % v] = mark(vec.tensor_copy(yo, src) if q == "v" else act.activation(yo, src, F.Copy))
         if v == r:
             wait("s", done["y%d" % v])
             count(syn.dma_start(T.y[r], yo), "d_y", 16)
+        if v == (NV - 1 if r in (3, 4) else r):
+            wait("s", done["y%d" % v])
             call = [c for c in CALLS if r in c][0]
             wait("s", ("arry", sum(len(shares(x, [d for d in call if d != x])[r]) for x in others(r))))
             for a, b in ((0, r), (r + 1, NV)):
@@ -405,36 +460,48 @@ def rank_program(g, core, T, topo):
     def join(n, name):
         a, b = {"": (0, 16), "a": (8, 16), "b": (0, 8)}[name[2:]]
         out = T.rj[:, 256 * n:256 * n + 256]
-        wait("v", done["jw%d" % n], c_js)
-        done[name] = mark(gather(out, T.jw[:, 160 * n:160 * n + 160], J + 1 + 2 * n, a, b))
+        wait("v", done["jw%d" % n], done["js%d" % n])
+        done[name] = mark(gather(out, T.jw[:, 160 * n:160 * n + 160], LATER[n], a, b))
         if a == 0:
             later.append(lambda: back(n, name))
 
     def back(n, name):
         wait("p", c_ee, done.get(name[0:2] + "a"), done[name])
+        if n == 1 and len(LATER) == 3:
+            wait("p", done["jw0"])
+            pe.matmul(T.po3[:, 0:128], T.rl[:, 0:128], T.rj[:, 256:512:2], True, False)
+            done["pjw2"] = mark(pe.matmul(T.po3[:, 0:128], T.rl[:, 8:136], T.rj[:, 257:512:2], False, True))
         for u in range(16):
-            last = pe.matmul((T.pj, T.pq)[n][:, 0:16], T.ee[:, 15 - u:143 - u], T.rj[:, 256 * n + u:256 * n + 256:16], u == 0, u == 15)
+            last = pe.matmul(T[jbanks[n]][:, 0:16], T.ee[:, 15 - u:143 - u], T.rj[:, 256 * n + u:256 * n + 256:16], u == 0, u == 15)
         done["back%d" % n] = mark(last)
 
-    def list_window():
-        wait("p", c_pick, done["lf"])
+    def list_window(k):
+        wait("p", c_pick, *got(EARLIER[k]))
         for n in range(8):
-            last = pe.matmul(T.po3[:, n:384:8], T.pick[:, 128 * n:128 * n + 128], T.lf[:], True, True)
-        done["pjw"] = mark(last)
+            last = pe.matmul((T.po3, T.pq)[k][:, n:128:8], T.pick[:, 128 * n:128 * n + 128], T.lf[:, 16 * k:16 * k + 16], True, True)
+        done["pjw%d" % k] = mark(last)
 
     later = []
 
     def on_vector(name):
-        if name == "low1":
-            done[name] = lows(1, 2)
-        elif name == "lows":
-            o = lows(2, NV)
-            for x in range(2, NV):
+        if name[0:3] == "low":
+            which = [int(c) for c in name[3:]]
+            o = lows(which)
+            for x in which:
                 done["low%d" % x] = o
-        elif name == "lf":
-            wait("v", *got(J))
-            done[name] = mark(vec.tensor_scalar(T.lf[:], T.lst[:, 16 * J:16 * J + 48], -1024.0, None, A.add))
-            later.append(list_window)
+        elif name[0:2] == "lf":
+            later.insert(0, lambda: list_window(int(name[2])))
+        elif name[0] == "u":
+            x = int(name[1])
+            k = EARLIER.index(x)
+            src = T.lf[:, 16 * k:16 * k + 16]
+            wait("v", *got(x))
+            whole(x, src, OFF[k])
+        elif name == "mwl":
+            done[name] = mark(vec.tensor_copy(T.mw[:, 7 * UW:8 * UW], T.mw[:, 0:UW]))
+        elif name == "mwm":
+            wait("v", o_mw)
+            done[name] = mark(vec.tensor_copy(T.mw[:, 8 * UW:MW], T.mw[:, 0:MW - 8 * UW]))
         elif name[0:3] == "lit":
             done[name] = twice(int(name[3]), (d_lt0, d_lt1)[int(name[3])])
         elif name[0] == "y":
@@ -443,71 +510,96 @@ def rank_program(g, core, T, topo):
             join(int(name[1]), name)
         elif name[0] == "c":
             n = int(name[1])
-            x, src = NV + n, (T.pj, T.pq)[n][:, 0:16]
+            x, src = NV + n, T[jbanks[n]][:, 0:16]
             wait("v", done["back%d" % n])
-            done["lst%d" % x] = mark(vec.tensor_scalar(T.lst[:, 16 * x:16 * x + 16], src, 1024.0, None, A.add))
-            done["low%d" % x] = mark(vec.tensor_scalar(T.low[:, 16 * x:16 * x + 16], src, 1016.5, 0.0625, A.add, A.mult))
+            whole(x, src, OFF[n])
         else:
             v = int(name[1])
             a, b = {"a": (8, 16), "b": (0, 8), name[1]: (0, 16)}[name[-1]]
-            done[name] = mark(version(v, v, v, a, b))
+            done[name] = mark(version(v, FROM[v][0], FROM[v][1], a, b))
             if name[-1] != "a":
                 rows(v, done[name], done.get(name[0:2] + "a"))
 
     def on_scalar(name):
         if name[0] == "Y":
             hand_on(int(name[1]), "a")
+        elif name == "js0":
+            wait("a", *o_col)
+            count(act.activation(T.jw[:, 128:144], T.fine[:, 0:16], F.Identity, bias=ja, scale=2.0), name)
+            done[name] = count(act.activation(T.jw[:, 144:160], T.fine[:, 0:16], F.Identity, bias=jb, scale=2.0), name)
+        elif name[0:2] == "js":
+            n = int(name[2])
+            wait("a", done["js0"])
+            done[name] = mark(act.activation(T.jw[:, 160 * n + 128:160 * n + 160], T.jw[:, 128:160], F.Identity,
+                                             bias=OFF[0] - OFF[n] + Q * (n - 1)))
         elif name[0] == "j":
             n = int(name[2])
-            wait("a", done["pjw"])
-            done[name] = mark(act.activation(T.jw[:, 160 * n:160 * n + 128], T.po3[:, 256 * n:256 * n + 128], F.Copy))
+            wait("a", done["pjw%d" % n])
+            done[name] = mark(act.activation(T.jw[:, 160 * n:160 * n + 128], (T.po3, T.pq, T.po3)[n][:, 0:128], F.Copy))
+        elif name == "mwm":
+            wait("a", o_mw)
+            done[name] = mark(act.activation(T.mw[:, 8 * UW:MW], T.mw[:, 0:MW - 8 * UW], F.Copy))
         else:
             x = int(name[1:])
             done[name] = [mask(x, 8, 16), mask(x, 0, 8)] if x in HALVES else [mask(x, 0, 16)]
 
-    for name in VFIRST:
+    vfirst, afirst, vslot, aslot = [[part.split() for part in x.split("/")] for x in PLAN[KIND[r]]]
+    for name in vfirst[0]:
         on_vector(name)
-    while later:
-        later.pop(0)()
-    for name in AFIRST:
+        while later:
+            later.pop(0)()
+    for name in afirst[0]:
         on_scalar(name)
     c_a = c_b = None
+
+    def literals(w):
+        for u in range(w, w + (WIN[w][1] - 128) // 32):
+            hf, at = (0, 32 * (u - 1)) if u <= 4 else (1, 32 * (u - 4))
+            wait("p", done["lit%d" % hf])
+            for a in range(0, 128, 32):
+                last = pe.matmul(T.pwa[a:a + 32, 64 + 32 * (u - w):96 + 32 * (u - w)], T.lrep[:, 32 * hf:32 * hf + 32],
+                                 T.ident[:, at:at + 32], True, True)
+        return last
+
+    if "lit0" in done:
+        literals(1)
     for k, (v, x, w, nxt) in enumerate(CHAIN):
         res = 256 * v
-        if nxt is None:
-            rows(v, mark(version(v, x, w, 0, 16)))
-            hand_on(v)
-            break
         g_1 = count(version(v, x, w, 8, 16), "g1")
         g_2 = count(version(v, x, w, 0, 8), "g2")
         at, n = WIN[nxt][0], WIN[nxt][1] - 128
-        wait("p", c_a)
-        for u in range(nxt, nxt + n // 32):
-            wait("p", done["lit%d" % (u // 4)])
-            for a in range(0, 128, 32):
-                pe.matmul(T.pwa[a:a + 32, 64 + 32 * (u - nxt):96 + 32 * (u - nxt)], T.lrep[:, 32 * (u // 4):32 * (u // 4) + 32],
-                          T.ident[:, 32 * (u % 4):32 * (u % 4) + 32], True, True)
         wait("p", g_1)
         pe.matmul(T.pwa[:, 0:64], T.rl[:, 0:128], T.res[:, res + 128:res + 256:2], True, False)
         p_a = count(pe.matmul(T.pwa[:, 0:64], T.rl[:, 8:136], T.res[:, res + 129:res + 256:2], False, True), "pa")
         wait("p", g_2, c_b)
         pe.matmul(T.pwb[:, 0:64], T.rl[:, 0:128], T.res[:, res:res + 128:2], True, False)
         p_b = count(pe.matmul(T.pwb[:, 0:64], T.rl[:, 8:136], T.res[:, res + 1:res + 128:2], False, True), "pb")
+        if "lit0" not in done:
+            on_vector("lit0")
+            wait("a", mark(literals(1)))
         rows(v)
         wait("a", p_a)
         c_a = count(act.activation(T.win[:, at + 64:at + 128 + n], T.pwa[:, 0:64 + n], F.Copy), "ca")
-        cut = VSLOT[k].index("|")
-        for name in VSLOT[k][:cut]:
+        cut = vslot[k].index("|")
+        for name in vslot[k][:cut]:
             on_vector(name)
         wait("v", p_b)
         c_b = count(vec.tensor_copy(T.win[:, at:at + 64], T.pwb[:, 0:64]), "cb")
         made[nxt] = [c_a, c_b]
-        for name in VSLOT[k][cut + 1:]:
+        for name in vslot[k][cut + 1:]:
             on_vector(name)
+        if k + 1 < len(CHAIN) and (r, k) in LITFIRST:
+            wait("p", c_a)
+            literals(CHAIN[k + 1][3])
         while later:
             later.pop(0)()
-        for name in ASLOT[k]:
+        if k + 1 < len(CHAIN) and (r, k) not in LITFIRST:
+            wait("p", c_a)
+            literals(CHAIN[k + 1][3])
+        for name in aslot[k]:
             on_scalar(name)
+    for name in vslot[len(CHAIN)]:
+        (on_scalar if name[0] in "Ym" else on_vector)(name)
     wait("g", ("loc", total["loc"]))
     for name in total:
         if waited.get(name, 0) < total[name]:

from concourse.bass import DstId, RemoteDMATransfer
from concourse.mybir import dt, AluOpType, AxisListType, ActivationFunctionType

NV = 8
S = 2048
Q = 512
BW = 36
UW = 384
MW = S + 2 * Q
AT = {x: 16 * n for n, x in enumerate((0, 4, 1, 2, 6, 7, 3, 5, 8, 9))}
YBANKS = ["po0", "po1", "po2", "pq", "pj", "po0", "po3", "pwb"]
OFF = (1024.0, 1024.0)
EARLIER = (3, 5)
LATER = (4, 6)
FROM = {3: (3, 3), 5: (5, 5), 7: (7, 7)}
J = 3
BIG128 = float(3 * 2 ** 29)
BIG32 = float(3 * 2 ** 27)
WIN = {1: (0, 160), 2: (160, 160), 3: (320, 192), 5: (512, 192), 7: (704, 160)}
CHAIN = [(0, 0, 0, 1), (1, 1, 1, 2), (2, 2, 2, 3), (4, 8, 3, 5), (6, 9, 5, 7)]
HALVES = (8, 9)
NA, NB = 3, 3
LTFIRST = True
WHOLE = ()
CALLS = [[v] for v in range(NV)]
ORDER = [[2, 1, 3, 0] if v in (3, 4) else [0, 1, 2, 3] for v in range(NV)]
LAG = 2
REP = 2
LMA = ()
LITFIRST = ()
EARLY = [4] + [2] * 7
KIND = [3, 1, 0, 0, 0, 0, 0, 2]
VS = "lf1 j0 low1267 | u3 / j1 | c0 / u5 y0 c1 | lit1 / v3 | y4 / v5 | y6 / v7 Y5 y7"
V0 = "lf0 j1 low412 | u5 / j0 | u3 / c1 c0 low7 y0 | lit1 / v3 | y4 / v5 | y6 / v7 Y5 y7"
AS = "m6 jw1 m2 / m3 m8 / m9 Y1 Y2 / m5 Y3 m7 / "
A0 = "m4 jw0 m2 / m5 m3 / m8 Y1 m9 / Y2 Y3 m7 / "
PLAN = [("lf0 mwl lit0 low4", "js0 js1 m4 jw0 m1", VS, AS),
        ("mwl lf1 low6 lit0", "js0 js1 m6 jw1 m1", V0, A0),
        ("mwl lit0 lf0 low4", "js0 js1 m4 jw0 m1", VS, AS),
        ("mwl lf1 low6", "js0 js1 m6 jw1 m1", V0, A0)]

SCRATCH = {
    "lni": ("sbuf", [128, 64], "int32"),
    "fri": ("sbuf", [128, 64], "int32"),
    "zf": ("sbuf", [128, 64], "float32"),
    "xx": ("sbuf", [128, 576], "float16"),
    "one": ("sbuf", [128, 128], "bfloat16"),
    "sel": ("sbuf", [128, 8], "bfloat16"),
    "seln": ("sbuf", [128, 8], "bfloat16"),
    "fine": ("sbuf", [128, 128], "bfloat16"),
    "rr": ("sbuf", [128, 48], "bfloat16"),
    "thr": ("sbuf", [128, 48], "bfloat16"),
    "krow": ("sbuf", [128, 48], "bfloat16"),
    "chalf": ("sbuf", [128, 128], "bfloat16"),
    "seed": ("sbuf", [128, 16], "bfloat16"),
    "cc": ("sbuf", [128, UW // 16], "bfloat16"),
    "cols": ("sbuf", [128, 8], "float32"),
    "colb": ("sbuf", [128, 16], "bfloat16"),
    "lp": ("sbuf", [128, 512], "bfloat16"),
    "lm": ("sbuf", [128, 512], "bfloat16"),
    "bf": ("sbuf", [128, 4 * BW], "float16"),
    "be": ("sbuf", [128, 4 * BW], "float16"),
    "snd": ("sbuf", [128, 4 * 40], "uint16"),
    "sndf": ("sbuf", [128, 4 * 40], "float16"),
    "lst": ("sbuf", [128, 176], "uint16"),
    "low": ("sbuf", [128, 176], "uint16"),
    "rep": ("sbuf", [128, UW // 16], "uint16"),
    "mw": ("sbuf", [128, MW], "bfloat16"),
    "ident": ("sbuf", [128, 128], "bfloat16"),
    "rlh": ("sbuf", [128, 16], "bfloat16"),
    "rl": ("sbuf", [128, 160], "bfloat16"),
    "w0": ("sbuf", [128, Q], "int32"),
    "lt0": ("sbuf", [128, 16], "int32"),
    "lt1": ("sbuf", [128, 16], "int32"),
    "lrep": ("sbuf", [128, 64], "bfloat16"),
    "win": ("sbuf", [128, 864], "bfloat16"),
    "msk": ("sbuf", [128, 11 * 256], "bfloat16"),
    "res": ("sbuf", [128, NV * 256], "bfloat16"),
    "yo": ("sbuf", [128, NV * 16], "float32"),
    "frow": ("sbuf", [128, 128], "bfloat16"),
    "pick": ("sbuf", [128, 1024], "bfloat16"),
    "ee": ("sbuf", [128, 144], "bfloat16"),
    "eh": ("sbuf", [128, 16], "bfloat16"),
    "lf": ("sbuf", [128, 48], "float16"),
    "jw": ("sbuf", [128, 480], "float32"),
    "rj": ("sbuf", [128, 768], "float16"),
    "stg": ("dram", [NV, 128, 4], "int32"),
    "land": ("dram", [NV, 128, 4], "int32"),
    "first": ("dram", [REP, 128, 4], "int32"),
    "yl": ("dram", [NV, 128, 16], "float32"),
    "pq": ("psum", [128, 512], "float32"),
    "po0": ("psum", [128, 512], "float32"),
    "po1": ("psum", [128, 512], "float32"),
    "po2": ("psum", [128, 512], "float32"),
    "po3": ("psum", [128, 512], "float32"),
    "pj": ("psum", [128, 512], "float32"),
    "pwa": ("psum", [128, 512], "float32"),
    "pwb": ("psum", [128, 512], "float32"),
}

NOPS = 104
SEMAPHORES = (["d_ln", "d_fr", "d_stg", "d_own", "d_w0", "d_lt0", "d_lt1", "d_y", "loc", "arrk0", "arrka", "arrkb",
               "arrl0", "arrl1", "arrl2", "arrl3", "arrl4", "arrl5", "arrl6", "arrl7", "arry",
               "g1", "g2", "pa", "pb", "ca", "cb", "mw", "lr0", "lr1", "sel", "thr", "pick", "js0", "w0", "iss", "f0", "f1", "f2", "f3"] + ["op%d" % k for k in range(NOPS)])


def rank_program(g, core, T, topo):
    r = T.rank_of(core)
    if r is None:
        return
    A = AluOpType
    F = ActivationFunctionType
    vec, act, pe, syn = g.vector, g.scalar, g.tensor, g.sync
    queues = {"g": g, "v": vec, "a": act, "p": pe, "s": syn}
    seen = {}
    waited = {}
    total = {}
    marks = []

    def wait(q, *deps):
        for d in deps:
            if d is not None and d[1] > 0 and seen.get((q, d[0]), 0) < d[1]:
                seen[(q, d[0])] = d[1]
                waited[d[0]] = max(waited.get(d[0], 0), d[1])
                queues[q].wait_ge(T.sem[d[0]], d[1])

    def count(ins, name, n=1):
        total[name] = total.get(name, 0) + n
        ins.then_inc(T.sem[name], n)
        return (name, total[name])

    def mark(ins):
        name = "op%d" % len(marks)
        marks.append(name)
        return count(ins, name)

    def shares(src, dests):
        eng = topo.engines(T.cores[src], T.cores[dests[0]])
        n = [1] * len(dests)
        k = len(dests) - 1
        while sum(n) + n[k] <= len(eng):
            n[k] *= 2
            k = (k - 1) % len(dests)
        out, at = {}, 0
        for d, m in zip(dests, n):
            out[d] = eng[at:at + m]
            at += m
        return out

    def others(src):
        return [d for d in range(NV) if d != src]

    def docs(src):
        return others(src) + [src]

    def pairs(src):
        out = []
        for b in ORDER[src]:
            two = docs(src)[2 * b:2 * b + 2]
            calls = [two[0:1], two[1:2]] if NV - 1 in two else [two]
            calls = [[d for d in c if d != src] for c in calls]
            out.append((b, [c for c in calls if c]))
        return out

    def send(pieces, engines, sem):
        tr = []
        for d, src, dst in pieces:
            rid, pid, _se = topo.addr(T.cores[d])
            dsts = dst if isinstance(dst, list) else [dst]
            tr.append(RemoteDMATransfer(dst_ids=[DstId(rid=rid, pnc=pid)] * len(dsts),
                                        dma_engine_mask=sum(1 << e for e in engines[d]),
                                        remote_sem=T.sem[sem], srcs=[src], dsts=dsts))
            total["loc"] = total.get("loc", 0) + len(engines[d])
        g.remote_dma_fused(tr, local_sem=T.sem.loc)

    def lit_calls(src):
        return [others(src)]

    def lit_share(src, dests):
        return shares(src, dests)

    def lit_in(vs):
        return sum(len(shares(v, others(v))[r]) * (REP if v == 0 else 1) for v in vs if v != r)

    def list_in(vs):
        return sum(len(shares(v, c)[r]) for v in vs if v != r for _b, calls in pairs(v) for c in calls if r in c)

    def lit_sem(v):
        return "arrk0" if v == 0 else "arrka" if v <= 4 else "arrkb"

    def list_sem(v):
        return "arrl%d" % v

    d_stg = count(syn.dma_start(T.stg[:], T.lit[:]), "d_stg", 16)
    d_ln = count(act.dma_start(T.lni[0:8, :], T.ln[:]), "d_ln", 16)
    d_fr = count(syn.dma_start(T.fri[0:8, :], T.frm[:]), "d_fr", 16)
    d_own = count(syn.dma_start(T.land[r], T.lit[r]), "d_own", 16)

    def xs(k, a=0, b=64):
        return T.xx[0:8, 64 + 128 * k + a:64 + 128 * k + b]

    XF, XE, XT, XM = 0, 1, 2, 3
    imp = {"allow_small_or_imprecise_dtypes": True}
    m_one = mark(vec.memset(T.one[:], 1.0))
    zc, hc, uc, pc, ja, jb = [T.cols[:, k:k + 1] for k in range(6)]
    c_z = mark(g.iota(zc, [[0, 1]], -15 - 256, 2, **imp))
    c_fine = mark(g.iota(T.fine[:], [[1, 8], [8, 16]], -64, 0, **imp))
    c_rr = mark(g.iota(T.rr[:, 0:BW], [[0, 2], [128, 18]], -128, 0, **imp))
    wait("g", m_one)
    mine = docs(r)
    cuts = [i for i in range(NV) if i == 0 or mine[i] != mine[i - 1] + 1] + [NV]
    for a, b in zip(cuts, cuts[1:]):
        c_sel = count(g.affine_select(T.sel[0:8, a:b], T.one[0:8, a:b], [[-1, b - a]], A.is_equal, 0.0, -mine[a], 1), "sel")
    m_c0 = mark(vec.memset(T.cc[:], 16.0))
    m_xx = mark(vec.memset(T.xx[0:8, :], 0.0))
    wait("v", c_z)
    o_h = mark(vec.tensor_scalar(hc, zc, BIG32, -BIG32, A.add, A.add))
    wait("v", m_xx)
    m_t0 = mark(vec.memset(xs(XT, 0, 1), -64.0))
    m_e0 = mark(vec.memset(xs(XE, 0, 1), (S if r == 0 else 0) - 1280.0))
    wait("v", o_h)
    o_u = mark(vec.tensor_scalar(uc, zc, hc, -1.0, A.subtract, A.add))
    wait("v", c_fine, m_c0)
    o_rs = mark(vec.tensor_scalar(T.rlh[:], T.fine[:, 0:16], 4.0, hc, A.mult, A.is_equal))
    wait("v", o_u)
    o_seed = mark(vec.tensor_scalar(T.seed[:], T.fine[:, 0:16], 0.25, uc, A.mult, A.is_equal))
    o_rep = mark(vec.tensor_scalar(T.rep[:], T.cc[:], uc, 0.5, A.add, A.mult))
    count(vec.memset(T.w0[:, 0:Q // 2], 0), "w0")
    wait("a", m_one)
    m_zf = mark(act.activation(T.zf[0:8, :], T.one[0:8, 0:64], F.Copy, scale=0.0))
    m_ch = mark(act.activation(T.chalf[0:1, :], T.one[0:1, 0:128], F.Copy, scale=-3.5))
    count(act.activation(T.thr[0:64, 18:BW], T.one[0:64, 0:18], F.Copy, scale=-1024.0), "thr")
    count(act.activation(T.thr[64:128, 0:18], T.one[64:128, 0:18], F.Copy, scale=-1024.0), "thr")
    wait("a", c_rr)
    m_kr = mark(act.activation(T.krow[0:1, 0:BW], T.rr[0:1, 0:BW], F.Identity, bias=128.0))
    count(act.activation(T.thr[0:64, 0:18], T.rr[0:64, 0:18], F.Copy), "thr")
    m_th = count(act.activation(T.thr[64:128, 18:BW], T.rr[64:128, 18:BW], F.Copy), "thr")
    wait("a", c_sel)
    m_sn = mark(act.activation(T.seln[0:8, :], T.sel[0:8, :], F.Copy, scale=-1.0))
    wait("a", o_seed, o_rep, o_rs)
    a_mw0 = mark(act.activation(T.mw[:, 0:UW], T.seed[:].indirect(T.rep[:]), F.Copy))
    c_rl = mark(act.activation(T.rl[:], T.rlh[:].indirect(T.rep[:, 0:10]), F.Copy))

    wait("g", d_stg)
    for dests in lit_calls(r):
        send([(d, T.stg[d], [T.first[n] for n in range(REP)] if r == 0 else T.land[r]) for d in dests],
             lit_share(r, dests), lit_sem(r))

    wait("v", d_ln, m_zf, m_t0)
    o_t = mark(vec.tensor_tensor_scan(xs(XT, 1, 64), T.lni[0:8, 0:63], T.zf[0:8, 0:63], -64.0, A.add, A.add))
    wait("v", d_fr)
    o_xf = mark(vec.tensor_scalar(xs(XF), T.fri[0:8, :], -1280.0, None, A.add))
    wait("v", o_t)
    o_xm = mark(vec.tensor_scalar(xs(XM), xs(XT), BIG128, -BIG128, A.add, A.add))
    wait("v", o_xf, m_e0)
    o_xe = mark(vec.tensor_tensor(xs(XE, 1, 64), xs(XF, 0, 63), T.lni[0:8, 0:63], A.add))
    wait("p", c_fine, m_one, m_ch)
    pe.matmul(T.pwb[:, 0:1], T.fine[0:1, :], T.one[0:1, 0:1], True, False)
    p_col = mark(pe.matmul(T.pwb[:, 0:1], T.chalf[0:1, :], T.one[0:1, 0:1], False, True))

    wait("p", m_kr)
    for b in range(4):
        pe.matmul(T["po%d" % b][:, 0:BW], T.one[0:1, 0:128], T.krow[0:1, 0:BW], True, False)

    def turn(col, k, sel, start, stop):
        ps = T.pq[:, 4 * col:4 * col + 4]
        pe.matmul(ps, T.xx[0:8, 64 + 128 * k:192 + 128 * k], sel[0:8, 0:8:2], start, False)
        return pe.matmul(ps, T.xx[0:8, 128 * k:128 + 128 * k], sel[0:8, 1:8:2], False, stop)

    single = r == 0
    wait("p", c_sel, m_sn, m_xx, o_t, m_t0)
    turn(XT, XT, T.sel, True, False)
    wait("p", o_xm)
    turn(XT, XM, T.seln, False, True)
    turn(XM, XM, T.sel, True, True)
    if not single:
        wait("p", o_xf)
        turn(XF, XF, T.sel, True, True)
    if single:
        wait("p", o_xf)
        turn(XF, XF, T.sel, True, False)
    wait("p", o_xe, m_e0)
    p_k = mark(turn(XF if single else XE, XE, T.seln, not single, True))

    m_w0 = count(vec.memset(T.w0[:, Q // 2:Q], 0), "w0")
    wait("v", p_col)
    o_pb = mark(vec.tensor_copy(T.colb[:, 8:9], T.pwb[:, 0:1]))
    o_col = [mark(vec.tensor_scalar(ja, uc, 0.5, 1672.0, A.mult, A.add)),
             mark(vec.tensor_scalar(jb, uc, 0.5, 1672.0 + 256, A.mult, A.add))]

    def turned():
        wait("s", d_own, ("arrka", lit_in([1, 2, 3, 4])))
        return count(syn.dma_start(T.lt0[:], T.land[1:5]), "d_lt0", 16)

    if LTFIRST and r > 0:
        d_lt0 = turned()
    wait("s", m_w0, d_own if r == 0 else ("arrk0", lit_in([0])))
    n = 1 if r == 0 else REP
    for h in range(0, 8, n):
        d_w0 = count(syn.dma_start(T.w0[16 * h:16 * (h + n - 1) + 1:16, :], T.land[0] if r == 0 else T.first[:]), "d_w0", 16)
    if EARLY[r] < 4:
        syn.sem_inc(T.sem.iss, 1)
    if not LTFIRST or r == 0:
        d_lt0 = turned()
    wait("s", ("arrkb", lit_in([5, 6, 7])))
    d_lt1 = count(syn.dma_start(T.lt1[:], T.land[4:8]), "d_lt1", 16)

    wait("v", p_k, m_th)
    o_sr = mark(vec.tensor_copy(T.colb[:, 0:4], T.pq[:, 4 * XT:4 * XT + 4]))
    p_out, o_snd = {}, []

    def factors(b):
        cols = slice(BW * b, BW * b + BW)
        now, old = slice(BW * b + 1, BW * b + BW), slice(BW * b, BW * b + BW - 1)
        xf, xe, sk = [T.pq[:, 4 * k + b:4 * k + b + 1] for k in (XF, XE, XM)]
        sr = T.colb[:, b:b + 1]
        lp, lm = T.lp[:, 128 * b:128 * b + 128], T.lm[:, 128 * b:128 * b + 128]
        name = "f%d" % b
        count(vec.tensor_scalar(T.bf[:, cols], T.thr[:, 0:BW], sk, xf, A.is_ge, A.mult), name)
        if single:
            count(vec.tensor_scalar(T.be[:, cols], T.thr[:, 0:BW], sk, xf, A.is_equal, A.mult), name)
            wait("v", o_sr)
            made = count(vec.tensor_scalar(lp, T.fine[:], sr, None, A.is_ge), name)
            prods = [(T.one[:, 0:128], T.bf[:, old]), (lp, T.be[:, now])]
        else:
            count(vec.tensor_scalar(T.be[:, cols], T.thr[:, 0:BW], sk, xe, A.is_ge, A.mult), name)
            wait("v", o_sr)
            made = count(vec.tensor_scalar(lp, T.fine[:], sr, None, A.is_ge), name)
            if r in LMA:
                wait("a", made)
                more = mark(act.activation(lm, lp, F.Identity, bias=1.0, scale=-1.0))
            else:
                made = count(vec.tensor_scalar(lm, T.fine[:], sr, None, A.is_lt), name)
            prods = [(lp, T.bf[:, now]), (lp, T.be[:, now]), (lm, T.bf[:, old]), (lm, T.be[:, old])]
        wait("p", made)
        for k, (left, right) in enumerate(prods):
            if k == 2 and r in LMA:
                wait("p", more)
            last = pe.matmul(T["po%d" % b][:, 0:BW - 1], left, right, False, k == len(prods) - 1)
        p_out[b] = mark(last)

    def as_list(out, b, a, n):
        return mark(vec.tensor_scalar(out, T["po%d" % b][:, a:a + n], T.pwb[:, 0:1], 67.5 - less, A.add, A.add))

    early = r in EARLIER
    less = OFF[EARLIER.index(r)] if early else 0.0
    snd = T.sndf if early else T.snd
    home = T.lf[:, 16 * EARLIER.index(r):16 * EARLIER.index(r) + 16] if early else T.lst[:, AT[r]:AT[r] + 16]

    def hand_out(b, calls):
        wait("v", p_out[b])
        o_snd.append(as_list(snd[:, 40 * b:40 * b + 34], b, 0, 34))
        wait("g", o_snd[-1])
        for dests in calls:
            at = {d: 40 * b + 18 * (mine.index(d) % 2) for d in dests}
            send([(d, snd[:, at[d]:at[d] + 16], home) for d in dests], shares(r, dests), list_sem(r))

    plan = pairs(r)
    lag = 2 if single else LAG
    for n in range(4 + lag):
        if n < 4:
            factors(plan[n][0])
        if n - lag == EARLY[r]:
            wait("g", ("iss", 1))
        if n - lag == 3:
            wait("v", a_mw0)
            count(vec.tensor_copy(T.mw[:, 6 * UW:7 * UW], T.mw[:, 0:UW]), "mw")
        if n >= lag:
            hand_out(*plan[n - lag])
    o_own = as_list(home, mine.index(r) // 2, 18 * (mine.index(r) % 2), 16)

    c_fr = mark(act.activation(T.frow[:], T.fine[:, 0:16].indirect(T.rep[:, 0:8]), F.Identity, bias=-59.5, scale=0.125))
    wait("a", a_mw0)
    for n in range(1, 1 + NA):
        count(act.activation(T.mw[:, UW * n:UW * n + UW], T.mw[:, 0:UW], F.Copy), "mw")
    wait("v", a_mw0, c_fr, o_pb)
    for n in range(1 + NA, 6):
        o_mw = count(vec.tensor_copy(T.mw[:, UW * n:UW * n + UW], T.mw[:, 0:UW]), "mw")
    for n in range(8):
        c_pick = count(vec.tensor_scalar(T.pick[:, 128 * n:128 * n + 128], T.frow[:], 16.0 * n, T.colb[:, 8:9],
                                         A.add, A.is_equal), "pick")
    c_id = mark(g.affine_select(T.ident[:], T.one[:], [[-1, 128]], A.is_equal, 0.0, 0, 1))
    m_ee = mark(g.iota(T.ee[:], [[0, 144]], 0, 0, **imp))
    c_e1 = mark(g.affine_select(T.eh[:, 0:9], T.one[:, 0:9], [[-16, 9]], A.is_ge, 0.0, 0, 1))
    wait("g", m_ee, c_e1)
    c_ee = mark(g.affine_select(T.ee[:, 15:144:16], T.eh[:, 0:9], [[16, 9]], A.is_ge, 0.0, 15, -1))

    def twice(hf, dma):
        wait("v", dma)
        for n in range(2):
            made = count(vec.tensor_copy(T.lrep[:, 32 * hf + 16 * n:32 * hf + 16 * n + 16], T["lt%d" % hf][:]), "lr%d" % hf)
        return made

    def got(*vs):
        return [o_own if v == r else (list_sem(v), list_in([v])) for v in vs]

    done = {}
    made = {}
    ybanks, jbanks = YBANKS, ["pj", "pq", "po3"][0:len(LATER)]
    wait("p", o_own, *o_snd, c_id, c_rl)

    def mask(x, a, b):
        wait("a", o_mw, *(got(x) if x < NV else [done["mwl"]]), done["lst%d" % x] if x in EARLIER or x >= NV else None)
        return mark(act.activation(T.msk[:, 256 * x + 16 * a:256 * x + 16 * b],
                                   T.mw[:, 0:S + Q if x < NV else MW].indirect(T.lst[:, AT[x] + a:AT[x] + b]), F.Copy))

    def lows(xs):
        wait("v", *got(*xs))
        a, b = AT[xs[0]], AT[xs[-1]] + 16
        return mark(vec.tensor_scalar(T.low[:, a:b], T.lst[:, a:b], -7.5, 0.0625, A.add, A.mult))

    def whole(x, src, off):
        done["lst%d" % x] = mark(vec.tensor_scalar(T.lst[:, AT[x]:AT[x] + 16], src, off, None, A.add))
        done["low%d" % x] = mark(vec.tensor_scalar(T.low[:, AT[x]:AT[x] + 16], src, off - 7.5, 0.0625, A.add, A.mult))

    def gather(out, win, x, a, b):
        halves = done["m%d" % x]
        wait("v", done["low%d" % x], *(halves if b - a == 16 else halves[-1:] if a == 0 else halves[0:1]))
        return vec.tensor_tensor(out[:, 16 * a:16 * b], win.indirect(T.low[:, AT[x] + a:AT[x] + b]),
                                 T.msk[:, 256 * x + 16 * a:256 * x + 16 * b], A.mult)

    def version(v, x, w, a, b):
        out = T.res[:, 256 * v:256 * v + 256]
        if v == 0:
            wait("v", d_w0, *got(0))
            return vec.tensor_copy(out[:, 16 * a:16 * b], T.w0[:].indirect(T.lst[:, a:b]))
        wait("v", *made[w])
        return gather(out, T.win[:, WIN[w][0]:WIN[w][0] + WIN[w][1]], x, a, b)

    def rows(v, *deps):
        py = ybanks[v]
        wait("p", *deps, done["y0"] if v > 0 and py == ybanks[0] else None)
        if py in jbanks:
            x = NV + jbanks.index(py)
            wait("p", done["lst%d" % x], done["low%d" % x])
        py = T[py]
        pe.matmul(py[:, 0:8], T.res[:, 256 * v:256 * v + 256:2], T.rl[:, 0:8], True, True)
        done["p%d" % v] = mark(pe.matmul(py[:, 8:16], T.res[:, 256 * v + 1:256 * v + 256:2], T.rl[:, 0:8], True, True))

    def hand_on(v, q="v"):
        yo, src = T.yo[:, 16 * v:16 * v + 16], T[ybanks[v]][:, 0:16]
        wait(q, done["p%d" % v])
        done["y%d" % v] = mark(vec.tensor_copy(yo, src) if q == "v" else act.activation(yo, src, F.Copy))
        if v == r:
            wait("s", done["y%d" % v])
            count(syn.dma_start(T.y[r], yo), "d_y", 16)
        if v == (NV - 1 if r in (3, 4) else r):
            wait("s", done["y%d" % v])
            call = [c for c in CALLS if r in c][0]
            wait("s", ("arry", sum(len(shares(x, [d for d in call if d != x])[r]) for x in others(r))))
            for a, b in ((0, r), (r + 1, NV)):
                if a < b:
                    count(syn.dma_start(T.y[a:b], T.yl[a:b]), "d_y", 16)
        for call in CALLS:
            dests = [d for d in call if d != r]
            if v == call[-1] and dests:
                wait("g", *[done["y%d" % d] for d in dests])
                send([(d, T.yo[:, 16 * d:16 * d + 16], T.yl[r]) for d in dests], shares(r, dests), "arry")

    def join(n, name):
        a, b = {"": (0, 16), "a": (8, 16), "b": (0, 8)}[name[2:]]
        out = T.rj[:, 256 * n:256 * n + 256]
        wait("v", done["jw%d" % n], done["js%d" % n])
        done[name] = mark(gather(out, T.jw[:, 160 * n:160 * n + 160], LATER[n], a, b))
        if a == 0:
            later.append(lambda: back(n, name))

    def back(n, name):
        wait("p", c_ee, done.get(name[0:2] + "a"), done[name])
        if n == 1 and len(LATER) == 3:
            wait("p", done["jw0"])
            pe.matmul(T.po3[:, 0:128], T.rl[:, 0:128], T.rj[:, 256:512:2], True, False)
            done["pjw2"] = mark(pe.matmul(T.po3[:, 0:128], T.rl[:, 8:136], T.rj[:, 257:512:2], False, True))
        for u in range(16):
            last = pe.matmul(T[jbanks[n]][:, 0:16], T.ee[:, 15 - u:143 - u], T.rj[:, 256 * n + u:256 * n + 256:16], u == 0, u == 15)
        done["back%d" % n] = mark(last)

    def list_window(k):
        wait("p", c_pick, *got(EARLIER[k]))
        for n in range(8):
            last = pe.matmul((T.po3, T.pq)[k][:, n:128:8], T.pick[:, 128 * n:128 * n + 128], T.lf[:, 16 * k:16 * k + 16], True, True)
        done["pjw%d" % k] = mark(last)

    later = []

    def on_vector(name):
        if name[0:3] == "low":
            which = [int(c) for c in name[3:]]
            o = lows(which)
            for x in which:
                done["low%d" % x] = o
        elif name[0:2] == "lf":
            later.insert(0, lambda: list_window(int(name[2])))
        elif name[0] == "u":
            x = int(name[1])
            k = EARLIER.index(x)
            src = T.lf[:, 16 * k:16 * k + 16]
            wait("v", *got(x))
            whole(x, src, OFF[k])
        elif name == "mwl":
            done[name] = mark(vec.tensor_copy(T.mw[:, 7 * UW:8 * UW], T.mw[:, 0:UW]))
        elif name == "mwm":
            wait("v", o_mw)
            done[name] = mark(vec.tensor_copy(T.mw[:, 8 * UW:MW], T.mw[:, 0:MW - 8 * UW]))
        elif name[0:3] == "lit":
            done[name] = twice(int(name[3]), (d_lt0, d_lt1)[int(name[3])])
        elif name[0] == "y":
            hand_on(int(name[1]))
        elif name[0] == "j":
            join(int(name[1]), name)
        elif name[0] == "c":
            n = int(name[1])
            x, src = NV + n, T[jbanks[n]][:, 0:16]
            wait("v", done["back%d" % n])
            whole(x, src, OFF[n])
        else:
            v = int(name[1])
            a, b = {"a": (8, 16), "b": (0, 8), name[1]: (0, 16)}[name[-1]]
            done[name] = mark(version(v, FROM[v][0], FROM[v][1], a, b))
            if name[-1] != "a":
                rows(v, done[name], done.get(name[0:2] + "a"))

    def on_scalar(name):
        if name[0] == "Y":
            hand_on(int(name[1]), "a")
        elif name == "js0":
            wait("a", *o_col)
            count(act.activation(T.jw[:, 128:144], T.fine[:, 0:16], F.Identity, bias=ja, scale=2.0), name)
            done[name] = count(act.activation(T.jw[:, 144:160], T.fine[:, 0:16], F.Identity, bias=jb, scale=2.0), name)
        elif name[0:2] == "js":
            n = int(name[2])
            wait("a", done["js0"])
            done[name] = mark(act.activation(T.jw[:, 160 * n + 128:160 * n + 160], T.jw[:, 128:160], F.Identity,
                                             bias=OFF[0] - OFF[n] + Q * (n - 1)))
        elif name[0] == "j":
            n = int(name[2])
            wait("a", done["pjw%d" % n])
            done[name] = mark(act.activation(T.jw[:, 160 * n:160 * n + 128], (T.po3, T.pq, T.po3)[n][:, 0:128], F.Copy))
        elif name == "mwm":
            wait("a", o_mw)
            done[name] = mark(act.activation(T.mw[:, 8 * UW:MW], T.mw[:, 0:MW - 8 * UW], F.Copy))
        else:
            x = int(name[1:])
            done[name] = [mask(x, 8, 16), mask(x, 0, 8)] if x in HALVES else [mask(x, 0, 16)]

    vfirst, afirst, vslot, aslot = [[part.split() for part in x.split("/")] for x in PLAN[KIND[r]]]
    for name in vfirst[0]:
        on_vector(name)
        while later:
            later.pop(0)()
    for name in afirst[0]:
        on_scalar(name)
    c_a = c_b = None

    def literals(w):
        for u in range(w, w + (WIN[w][1] - 128) // 32):
            hf, at = (0, 32 * (u - 1)) if u <= 4 else (1, 32 * (u - 4))
            wait("p", done["lit%d" % hf])
            for a in range(0, 128, 32):
                last = pe.matmul(T.pwa[a:a + 32, 64 + 32 * (u - w):96 + 32 * (u - w)], T.lrep[:, 32 * hf:32 * hf + 32],
                                 T.ident[:, at:at + 32], True, True)
        return last

    if "lit0" in done:
        literals(1)
    for k, (v, x, w, nxt) in enumerate(CHAIN):
        res = 256 * v
        g_1 = count(version(v, x, w, 8, 16), "g1")
        g_2 = count(version(v, x, w, 0, 8), "g2")
        at, n = WIN[nxt][0], WIN[nxt][1] - 128
        wait("p", g_1)
        pe.matmul(T.pwa[:, 0:64], T.rl[:, 0:128], T.res[:, res + 128:res + 256:2], True, False)
        p_a = count(pe.matmul(T.pwa[:, 0:64], T.rl[:, 8:136], T.res[:, res + 129:res + 256:2], False, True), "pa")
        wait("p", g_2, c_b)
        pe.matmul(T.pwb[:, 0:64], T.rl[:, 0:128], T.res[:, res:res + 128:2], True, False)
        p_b = count(pe.matmul(T.pwb[:, 0:64], T.rl[:, 8:136], T.res[:, res + 1:res + 128:2], False, True), "pb")
        if "lit0" not in done:
            on_vector("lit0")
            wait("a", mark(literals(1)))
        rows(v)
        wait("a", p_a)
        c_a = count(act.activation(T.win[:, at + 64:at + 128 + n], T.pwa[:, 0:64 + n], F.Copy), "ca")
        cut = vslot[k].index("|")
        for name in vslot[k][:cut]:
            on_vector(name)
        wait("v", p_b)
        c_b = count(vec.tensor_copy(T.win[:, at:at + 64], T.pwb[:, 0:64]), "cb")
        made[nxt] = [c_a, c_b]
        for name in vslot[k][cut + 1:]:
            on_vector(name)
        if k + 1 < len(CHAIN) and (r, k) in LITFIRST:
            wait("p", c_a)
            literals(CHAIN[k + 1][3])
        while later:
            later.pop(0)()
        if k + 1 < len(CHAIN) and (r, k) not in LITFIRST:
            wait("p", c_a)
            literals(CHAIN[k + 1][3])
        for name in aslot[k]:
            on_scalar(name)
    for name in vslot[len(CHAIN)]:
        (on_scalar if name[0] in "Ym" else on_vector)(name)
    wait("g", ("loc", total["loc"]))
    for name in total:
        if waited.get(name, 0) < total[name]:
            wait("s", (name, total[name]))
